import numpy as np
import ml_dtypes


def mxq(x, axis, fmt="e4m3"):
    dtype, down = {"e4m3": (ml_dtypes.float8_e4m3fn, 7), "e5m2": (ml_dtypes.float8_e5m2, 14)}[fmt]
    v = np.moveaxis(np.asarray(x, np.float32).astype(ml_dtypes.bfloat16).astype(np.float64), axis, -1)
    blocks = v.reshape(v.shape[:-1] + (-1, 32))
    amax = np.abs(blocks).max(-1, keepdims=True)
    byte = np.maximum(np.where(amax > 0, np.frexp(amax)[1] - 1 + 127, 0) - down, 1)
    scale = np.exp2(byte - 127.0)
    codes = (blocks / scale).astype(np.float32).astype(dtype).astype(np.float64)
    return np.moveaxis((codes * scale).reshape(v.shape), -1, axis)


WIDE = False


def mx_kscale(k):
    if not WIDE:
        return np.ones(k)
    levels = np.array([10, -10, 5, -5, 0])
    if k % 512:
        return np.exp2(np.random.permutation(np.resize(levels, k // 32))).repeat(32)
    a = np.empty((k // 512, 16))
    for p in range(k // 512):
        a[p, :8] = np.random.permutation(np.resize(levels, 8))
        for g in range(8):
            far = levels[np.abs(levels - a[p, g]) >= 10]
            a[p, g + 8] = far[np.random.randint(len(far))]
    return np.exp2(a.ravel()).repeat(32)


def f64(x):
    return np.asarray(x).astype(np.float64)


def striped(idx):
    return np.tile(idx.reshape(-1, 16).T, (8, 1)).astype(np.uint16)


def unstriped(offs):
    return offs[:16].T.reshape(-1).astype(np.int64)


def pack_weight(w):
    k, n = w.shape
    w = f64(np.asarray(w, np.float32).astype(ml_dtypes.bfloat16)).reshape(k // 32, 32, n)
    amax = np.abs(w).max(1)
    byte = np.clip(np.where(amax > 0, np.frexp(amax)[1] - 1 + 127 - 7, 1), 1, 254)
    scaled = (w * np.exp2(127.0 - byte)[:, None, :]).reshape(k, n).astype(np.float32)
    words = np.ascontiguousarray(scaled.reshape(k // 512, 128, 4, n).transpose(0, 1, 3, 2)).astype(ml_dtypes.float8_e4m3fn).view(np.uint8)
    return words, np.ascontiguousarray(byte.astype(np.uint8).reshape(k // 512, 16, n))


def unpack_weight(words, scales):
    g, p, n, _ = words.shape
    vals = np.ascontiguousarray(words).view(ml_dtypes.float8_e4m3fn).astype(np.float64) * np.repeat(np.exp2(scales.astype(np.float64) - 127.0), 8, axis=1)[..., None]
    return vals.transpose(0, 1, 3, 2).reshape(g * 512, n)


def relu(v):
    return np.maximum(v, 0.0)


K, T, S, N, D = 512, 1024, 512, 256, 2
P = 2 ** 7


def setup_inputs():
    n = np.random.standard_normal
    s = mx_kscale(K)[:, None]
    packed_xT = pack_weight(n((K, T)) * s)
    return {
        "x_words": packed_xT[0],
        "x_scales": packed_xT[1],
        "w1": (n((K, N)) / np.sqrt(K) / s).astype(np.float32),
        "gate": (np.tile(np.random.uniform(0.3, 0.6, (D, 1, S)), (1, P, 1))).astype(np.float32),
        "coef": (0.6 * n((N, 3)) + 0.3).astype(np.float32),
        "offs": striped(np.random.permutation(T)[:S]),
        "pos1": striped(np.random.permutation(S)[:S]),
        "pos2": striped(np.random.permutation(S)[:S]),
    }


def reference(x_words, x_scales, w1, gate, coef, offs, pos1, pos2):
    xq = unpack_weight(x_words, x_scales)[:, unstriped(offs)]
    h = relu(mxq(f64(w1), 0, "e4m3").T @ xq)
    gg = h[:, unstriped(pos1)] * f64(gate)[0, :1] + h[:, unstriped(pos2)] * f64(gate)[1, :1]
    ee = gg[:, unstriped(pos1)] * f64(gate)[0, :1] + gg[:, unstriped(pos2)] * f64(gate)[1, :1]
    return f64(coef)[:, 0:1] * h + f64(coef)[:, 1:2] * gg + f64(coef)[:, 2:3] * ee

@@ -1,0 +1,159 @@
+from contextlib import ExitStack
+
+import concourse.mybir as mybir
+from concourse.masks import make_identity
+
+K, T, S, N = 512, 1024, 512, 256
+P = 128
+PACK = 4
+PAD = 8
+FLOPS = 2 * K * S * N
+
+F32 = mybir.dt.float32
+BF16 = mybir.dt.bfloat16
+I32 = mybir.dt.int32
+U32 = mybir.dt.uint32
+U16 = mybir.dt.uint16
+U8 = mybir.dt.uint8
+FP8X4 = mybir.dt.float8_e4m3fn_x4
+MULT = mybir.AluOpType.mult
+ADD = mybir.AluOpType.add
+RELU = mybir.ActivationFunctionType.Relu
+COPY = mybir.ActivationFunctionType.Copy
+
+
+def tile_picked_ygpr_relu_p_kernel(tc, x_words, x_scales, w1, gate, coef, offs, pos1, pos2, out):
+    nc = tc.nc
+    blocks = range(N // P)
+    chunks = [slice(c * P, (c + 1) * P) for c in range(S // P)]
+
+    with ExitStack() as ctx:
+        sb = ctx.enter_context(tc.tile_pool(name="sb", bufs=1))
+        ps = ctx.enter_context(tc.psum_pool(name="ps", bufs=1))
+
+        def per_block(pool, name, shape, dtype):
+            return [pool.tile(shape, dtype, name="%s%d" % (name, b), align_bytes=64) for b in blocks]
+
+        offs_sb = sb.tile([P, S // 16], U16, name="offs_sb")
+        pos1_sb = sb.tile([P, S // 16], U16, name="pos1_sb")
+        pos2_sb = sb.tile([P, S // 16], U16, name="pos2_sb")
+        all_scales = sb.tile([P, T], U8, name="all_scales", align_bytes=64)
+        all_words = sb.tile([P, T], I32, name="all_words", align_bytes=64)
+        w_raw = sb.tile([P, PACK, N], F32, name="w_raw", align_bytes=64)
+        gates = per_block(sb, "gate", [P, S], F32)
+        coef_sb = sb.tile([P, N // P, 3], F32, name="coef_sb")
+        zeros = sb.tile([P, PAD], F32, name="zeros")
+        ident = sb.tile([P, P], F32, name="ident", align_bytes=64)
+
+        nc.gpsimd.memset(all_scales[:].bitcast(I32), 0)
+        nc.gpsimd.memset(zeros[:], 0.0)
+        nc.sync.dma_start(offs_sb[:], offs)
+        nc.sync.dma_start(w_raw[:], w1.rearrange("(p j) n -> p j n", j=PACK))
+        for q in range(4):
+            nc.scalar.dma_start(all_scales[32 * q : 32 * q + 4, :].bitcast(I32), x_scales[0, 4 * q : 4 * q + 4, :].bitcast(I32))
+        nc.sync.dma_start(all_words[:], x_words[0].rearrange("p n t -> p (n t)").bitcast(I32))
+        nc.sync.dma_start(pos1_sb[:], pos1)
+        nc.sync.dma_start(gates[0][:], gate[0])
+        nc.sync.dma_start(pos2_sb[:], pos2)
+        nc.sync.dma_start(gates[1][:], gate[1])
+        nc.sync.dma_start(coef_sb[:], coef.rearrange("(b p) c -> p b c", p=P))
+        make_identity(nc, ident[:])
+
+        h = per_block(sb, "h", [P, S + PAD], F32)
+        gg = per_block(sb, "gg", [P, S + PAD], F32)
+        for window in h + gg:
+            nc.scalar.activation(window[:, S:], zeros[:], RELU)
+
+        x_scale = sb.tile([P, S], U8, name="x_scale", align_bytes=64)
+        nc.vector.tensor_copy(x_scale[:], all_scales[:].indirect(offs_sb[:]))
+
+        w_bf = per_block(sb, "w_bf", [P, P, PACK], BF16)
+        w_code = per_block(sb, "w_code", [P, P], U32)
+        w_scale = per_block(sb, "w_scale", [P, P], U8)
+        for b in blocks:
+            nc.scalar.copy(
+                w_bf[b][:].rearrange("p (c i) t -> p c t i", i=4),
+                w_raw[:, :, b * P : (b + 1) * P].rearrange("p t (c i) -> p c t i", i=4),
+            )
+            nc.vector.quantize_mx(out=w_code[b][:].bitcast(FP8X4), scales=w_scale[b][:], in_=w_bf[b][:].rearrange("p m t -> p (m t)"))
+
+        x_code = sb.tile([P, S], U32, name="x_code", align_bytes=64)
+        for lo, hi in ((0, 384), (384, S)):
+            nc.vector.tensor_copy(x_code[:, lo:hi], all_words[:].bitcast(U32).indirect(offs_sb[:, lo // 16 : hi // 16]))
+
+        def project(acc, b, lo, hi):
+            nc.tensor.matmul_mx(
+                out=acc[:, lo:hi], lhsT=w_code[b][:].bitcast(FP8X4), lhsT_scale=w_scale[b][:],
+                rhs=x_code[:, lo:hi].bitcast(FP8X4), rhs_scale=x_scale[:, lo:hi], start=True, stop=True,
+            )
+
+        head = ps.tile([P, S], F32, name="head")
+        rest = ps.tile([P, S], F32, name="rest")
+        second = ps.tile([P, S], F32, name="second")
+        project(head, 0, 0, 256)
+        project(head, 0, 256, 384)
+        nc.scalar.activation(h[0][:, 0:384], head[:, 0:384], RELU)
+        project(rest, 0, 384, S)
+        nc.scalar.activation(h[0][:, 384:S], rest[:, 384:S], RELU)
+        project(second, 1, 0, S)
+        nc.scalar.activation(h[1][:, 0:S], second[:], RELU)
+
+        t1 = per_block(sb, "t1", [P, S], F32)
+        t2 = per_block(sb, "t2", [P, S], F32)
+        u1 = per_block(sb, "u1", [P, S], F32)
+        u2 = per_block(sb, "u2", [P, S], F32)
+        h_c = per_block(sb, "h_c", [P, S], F32)
+        gg_c = per_block(sb, "gg_c", [P, S], F32)
+        gate_c = per_block(sb, "gate_c", [P, S], F32)
+        turned_sb = per_block(sb, "turned_sb", [P, S], F32)
+        res = per_block(sb, "res", [P, S], F32)
+        turned = [ps.tile([P, S], F32, name="turned%d" % b) for b in blocks]
+        partial = [ps.tile([P, S], F32, name="partial%d" % b) for b in blocks]
+
+        def fetch(dst, window, pos, factor, lo=0, hi=S):
+            nc.vector.tensor_tensor(dst[:, lo:hi], window[:].indirect(pos[:, lo // 16 : hi // 16]), factor[:, lo:hi], MULT)
+
+        def scaled(dst, src, b, depth):
+            nc.scalar.activation(dst[:], src[:, 0:S], COPY, scale=coef_sb[:, b, depth : depth + 1])
+
+        def add_turned(b, term, first, last):
+            for c, cols in enumerate(chunks):
+                nc.tensor.matmul(turned[b][:, cols], term[:, cols], ident[:], is_transpose=True,
+                                 start=first and c == 0, stop=last and c == len(chunks) - 1)
+
+        def turn_back(b):
+            nc.scalar.copy(turned_sb[b][:], turned[b][:])
+            for cols in chunks:
+                nc.tensor.transpose(partial[b][:, cols], turned_sb[b][:, cols], ident[:])
+
+        def finish(b, lo, hi):
+            nc.vector.scalar_tensor_tensor(res[b][:, lo:hi], u2[b][:, lo:hi], coef_sb[:, b, 2:3], partial[b][:, lo:hi], MULT, ADD)
+            nc.sync.dma_start(out[b * P : (b + 1) * P, lo:hi], res[b][:, lo:hi])
+
+        fetch(t1[0], h[0], pos1_sb, gates[0])
+        fetch(t2[0], h[0], pos2_sb, gates[1])
+        for b in blocks:
+            scaled(gate_c[b], gates[0], b, 2)
+            scaled(h_c[b], h[b], b, 0)
+            add_turned(b, h_c[b], True, False)
+        fetch(t1[1], h[1], pos1_sb, gates[0])
+        nc.vector.tensor_tensor(gg[0][:, 0:S], t1[0][:], t2[0][:], ADD)
+        scaled(gg_c[0], gg[0], 0, 1)
+        add_turned(0, gg_c[0], False, False)
+        fetch(t2[1], h[1], pos2_sb, gates[1])
+        fetch(u1[0], gg[0], pos1_sb, gate_c[0])
+        add_turned(0, u1[0], False, True)
+        turn_back(0)
+        nc.vector.tensor_tensor(gg[1][:, 0:S], t1[1][:], t2[1][:], ADD)
+        scaled(gg_c[1], gg[1], 1, 1)
+        add_turned(1, gg_c[1], False, False)
+        fetch(u2[0], gg[0], pos2_sb, gates[1], 0, S // 2)
+        fetch(u1[1], gg[1], pos1_sb, gate_c[1])
+        add_turned(1, u1[1], False, True)
+        turn_back(1)
+        fetch(u2[0], gg[0], pos2_sb, gates[1], S // 2, S)
+        fetch(u2[1], gg[1], pos2_sb, gates[1], 0, S // 2)
+        finish(0, 0, S)
+        fetch(u2[1], gg[1], pos2_sb, gates[1], S // 2, S)
+        finish(1, 0, S // 2)
+        finish(1, S // 2, S)

@@ -40,23 +40,23 @@ def tile_picked_ygpr_relu_p_kernel(tc, x_words, x_scales, w1, gate, coef, offs, 
         all_scales = sb.tile([P, T], U8, name="all_scales", align_bytes=64)
         all_words = sb.tile([P, T], I32, name="all_words", align_bytes=64)
         w_raw = sb.tile([P, PACK, N], F32, name="w_raw", align_bytes=64)
-        gates = per_block(sb, "gate", [P, S], F32)
+        gate_sb = sb.tile([P, 2, S], F32, name="gate_sb", align_bytes=64)
+        gates = [gate_sb[:, d, :] for d in range(2)]
         coef_sb = sb.tile([P, N // P, 3], F32, name="coef_sb")
         zeros = sb.tile([P, PAD], F32, name="zeros")
         ident = sb.tile([P, P], F32, name="ident", align_bytes=64)
 
         nc.gpsimd.memset(all_scales[:].bitcast(I32), 0)
         nc.gpsimd.memset(zeros[:], 0.0)
+        nc.gpsimd.dma_start(coef_sb[:], coef.rearrange("(b p) c -> p b c", p=P))
         nc.sync.dma_start(offs_sb[:], offs)
-        nc.sync.dma_start(w_raw[:], w1.rearrange("(p j) n -> p j n", j=PACK))
-        for q in range(4):
-            nc.scalar.dma_start(all_scales[32 * q : 32 * q + 4, :].bitcast(I32), x_scales[0, 4 * q : 4 * q + 4, :].bitcast(I32))
         nc.sync.dma_start(all_words[:], x_words[0].rearrange("p n t -> p (n t)").bitcast(I32))
+        for q in range(4):
+            nc.sync.dma_start(all_scales[32 * q : 32 * q + 4, :].bitcast(I32), x_scales[0, 4 * q : 4 * q + 4, :].bitcast(I32))
+        nc.sync.dma_start(w_raw[:], w1.rearrange("(p j) n -> p j n", j=PACK))
+        nc.sync.dma_start(gate_sb[:], gate.rearrange("d p s -> p d s"))
         nc.sync.dma_start(pos1_sb[:], pos1)
-        nc.sync.dma_start(gates[0][:], gate[0])
         nc.sync.dma_start(pos2_sb[:], pos2)
-        nc.sync.dma_start(gates[1][:], gate[1])
-        nc.sync.dma_start(coef_sb[:], coef.rearrange("(b p) c -> p b c", p=P))
         make_identity(nc, ident[:])
 
         h = per_block(sb, "h", [P, S + PAD], F32)
@@ -64,39 +64,43 @@ def tile_picked_ygpr_relu_p_kernel(tc, x_words, x_scales, w1, gate, coef, offs, 
         for window in h + gg:
             nc.scalar.activation(window[:, S:], zeros[:], RELU)
 
-        x_scale = sb.tile([P, S], U8, name="x_scale", align_bytes=64)
-        nc.vector.tensor_copy(x_scale[:], all_scales[:].indirect(offs_sb[:]))
+        x_code = sb.tile([P, S], U32, name="x_code", align_bytes=64)
+        nc.vector.tensor_copy(x_code[:], all_words[:].bitcast(U32).indirect(offs_sb[:]))
 
-        w_bf = per_block(sb, "w_bf", [P, P, PACK], BF16)
         w_code = per_block(sb, "w_code", [P, P], U32)
         w_scale = per_block(sb, "w_scale", [P, P], U8)
-        for b in blocks:
+
+        def quantise(b):
+            w_bf = sb.tile([P, P, PACK], BF16, name="w_bf%d" % b, tag="staging%d" % b, align_bytes=64)
             nc.scalar.copy(
-                w_bf[b][:].rearrange("p (c i) t -> p c t i", i=4),
+                w_bf[:].rearrange("p (c i) t -> p c t i", i=4),
                 w_raw[:, :, b * P : (b + 1) * P].rearrange("p t (c i) -> p c t i", i=4),
             )
-            nc.vector.quantize_mx(out=w_code[b][:].bitcast(FP8X4), scales=w_scale[b][:], in_=w_bf[b][:].rearrange("p m t -> p (m t)"))
+            nc.vector.quantize_mx(out=w_code[b][:].bitcast(FP8X4), scales=w_scale[b][:], in_=w_bf[:].rearrange("p m t -> p (m t)"))
 
-        x_code = sb.tile([P, S], U32, name="x_code", align_bytes=64)
-        for lo, hi in ((0, 384), (384, S)):
-            nc.vector.tensor_copy(x_code[:, lo:hi], all_words[:].bitcast(U32).indirect(offs_sb[:, lo // 16 : hi // 16]))
+        half = S // 2
+        x_scale = [sb.tile([P, half], U8, name="x_scale0", align_bytes=64)]
+        nc.vector.tensor_copy(x_scale[0][:], all_scales[:].indirect(offs_sb[:, 0 : half // 16]))
+        quantise(0)
+        x_scale.append(sb.tile([P, half], U8, name="x_scale1", tag="staging0", align_bytes=64))
 
         def project(acc, b, lo, hi):
+            part = lo // half
             nc.tensor.matmul_mx(
                 out=acc[:, lo:hi], lhsT=w_code[b][:].bitcast(FP8X4), lhsT_scale=w_scale[b][:],
-                rhs=x_code[:, lo:hi].bitcast(FP8X4), rhs_scale=x_scale[:, lo:hi], start=True, stop=True,
+                rhs=x_code[:, lo:hi].bitcast(FP8X4), rhs_scale=x_scale[part][:, lo - part * half : hi - part * half], start=True, stop=True,
             )
 
-        head = ps.tile([P, S], F32, name="head")
-        rest = ps.tile([P, S], F32, name="rest")
-        second = ps.tile([P, S], F32, name="second")
-        project(head, 0, 0, 256)
-        project(head, 0, 256, 384)
-        nc.scalar.activation(h[0][:, 0:384], head[:, 0:384], RELU)
-        project(rest, 0, 384, S)
-        nc.scalar.activation(h[0][:, 384:S], rest[:, 384:S], RELU)
-        project(second, 1, 0, S)
-        nc.scalar.activation(h[1][:, 0:S], second[:], RELU)
+        for i, (lo, hi) in enumerate(((0, 256), (256, 384), (384, S))):
+            if lo >= half:
+                nc.vector.tensor_copy(x_scale[1][:, lo - half : hi - half], all_scales[:].indirect(offs_sb[:, lo // 16 : hi // 16]))
+            acc = ps.tile([P, S], F32, name="acc%d" % i)
+            project(acc, 0, lo, hi)
+            if hi < S:
+                nc.scalar.activation(h[0][:, lo:hi], acc[:, lo:hi], RELU)
+            else:
+                quantise(1)
+                nc.vector.tensor_scalar_max(h[0][:, lo:hi], acc[:, lo:hi], 0.0)
 
         t1 = per_block(sb, "t1", [P, S], F32)
         t2 = per_block(sb, "t2", [P, S], F32)
@@ -131,9 +135,14 @@ def tile_picked_ygpr_relu_p_kernel(tc, x_words, x_scales, w1, gate, coef, offs, 
             nc.sync.dma_start(out[b * P : (b + 1) * P, lo:hi], res[b][:, lo:hi])
 
         fetch(t1[0], h[0], pos1_sb, gates[0])
+        second = ps.tile([P, S], F32, name="second")
+        project(second, 1, 0, half)
+        project(second, 1, half, S)
+        nc.scalar.activation(h[1][:, 0:S], second[:], RELU)
         fetch(t2[0], h[0], pos2_sb, gates[1])
         for b in blocks:
             scaled(gate_c[b], gates[0], b, 2)
+        for b in blocks:
             scaled(h_c[b], h[b], b, 0)
             add_turned(b, h_c[b], True, False)
         fetch(t1[1], h[1], pos1_sb, gates[0])
@@ -141,19 +150,19 @@ def tile_picked_ygpr_relu_p_kernel(tc, x_words, x_scales, w1, gate, coef, offs, 
         scaled(gg_c[0], gg[0], 0, 1)
         add_turned(0, gg_c[0], False, False)
         fetch(t2[1], h[1], pos2_sb, gates[1])
-        fetch(u1[0], gg[0], pos1_sb, gate_c[0])
-        add_turned(0, u1[0], False, True)
-        turn_back(0)
+        fetch(u1[0], gg[0], pos1_sb, gate_c[0], 0, half)
         nc.vector.tensor_tensor(gg[1][:, 0:S], t1[1][:], t2[1][:], ADD)
         scaled(gg_c[1], gg[1], 1, 1)
         add_turned(1, gg_c[1], False, False)
-        fetch(u2[0], gg[0], pos2_sb, gates[1], 0, S // 2)
+        fetch(u1[0], gg[0], pos1_sb, gate_c[0], half, S)
+        add_turned(0, u1[0], False, True)
         fetch(u1[1], gg[1], pos1_sb, gate_c[1])
         add_turned(1, u1[1], False, True)
+        turn_back(0)
         turn_back(1)
-        fetch(u2[0], gg[0], pos2_sb, gates[1], S // 2, S)
-        fetch(u2[1], gg[1], pos2_sb, gates[1], 0, S // 2)
+        fetch(u2[0], gg[0], pos2_sb, gates[1])
+        fetch(u2[1], gg[1], pos2_sb, gates[1], 0, half)
         finish(0, 0, S)
-        fetch(u2[1], gg[1], pos2_sb, gates[1], S // 2, S)
-        finish(1, 0, S // 2)
-        finish(1, S // 2, S)
+        fetch(u2[1], gg[1], pos2_sb, gates[1], half, S)
+        finish(1, 0, half)
+        finish(1, half, S)

@@ -39,7 +39,7 @@ def tile_picked_ygpr_relu_p_kernel(tc, x_words, x_scales, w1, gate, coef, offs, 
         pos2_sb = sb.tile([P, S // 16], U16, name="pos2_sb")
         all_scales = sb.tile([P, T], U8, name="all_scales", align_bytes=64)
         all_words = sb.tile([P, T], I32, name="all_words", align_bytes=64)
-        w_raw = sb.tile([P, PACK, N], F32, name="w_raw", align_bytes=64)
+        w_raw = per_block(sb, "w_raw", [P, PACK, P], F32)
         gate_sb = sb.tile([P, 2, S], F32, name="gate_sb", align_bytes=64)
         gates = [gate_sb[:, d, :] for d in range(2)]
         coef_sb = sb.tile([P, N // P, 3], F32, name="coef_sb")
@@ -48,16 +48,17 @@ def tile_picked_ygpr_relu_p_kernel(tc, x_words, x_scales, w1, gate, coef, offs, 
 
         nc.gpsimd.memset(all_scales[:].bitcast(I32), 0)
         nc.gpsimd.memset(zeros[:], 0.0)
+        make_identity(nc, ident[:])
         nc.gpsimd.dma_start(coef_sb[:], coef.rearrange("(b p) c -> p b c", p=P))
         nc.sync.dma_start(offs_sb[:], offs)
         nc.sync.dma_start(all_words[:], x_words[0].rearrange("p n t -> p (n t)").bitcast(I32))
         for q in range(4):
             nc.sync.dma_start(all_scales[32 * q : 32 * q + 4, :].bitcast(I32), x_scales[0, 4 * q : 4 * q + 4, :].bitcast(I32))
-        nc.sync.dma_start(w_raw[:], w1.rearrange("(p j) n -> p j n", j=PACK))
-        nc.sync.dma_start(gate_sb[:], gate.rearrange("d p s -> p d s"))
+        for b in blocks:
+            nc.sync.dma_start(w_raw[b][:], w1.rearrange("(p j) n -> p j n", j=PACK)[:, :, b * P : (b + 1) * P])
         nc.sync.dma_start(pos1_sb[:], pos1)
         nc.sync.dma_start(pos2_sb[:], pos2)
-        make_identity(nc, ident[:])
+        nc.sync.dma_start(gate_sb[:], gate.rearrange("d p s -> p d s"))
 
         h = per_block(sb, "h", [P, S + PAD], F32)
         gg = per_block(sb, "gg", [P, S + PAD], F32)
@@ -74,7 +75,7 @@ def tile_picked_ygpr_relu_p_kernel(tc, x_words, x_scales, w1, gate, coef, offs, 
             w_bf = sb.tile([P, P, PACK], BF16, name="w_bf%d" % b, tag="staging%d" % b, align_bytes=64)
             nc.scalar.copy(
                 w_bf[:].rearrange("p (c i) t -> p c t i", i=4),
-                w_raw[:, :, b * P : (b + 1) * P].rearrange("p t (c i) -> p c t i", i=4),
+                w_raw[b][:].rearrange("p t (c i) -> p c t i", i=4),
             )
             nc.vector.quantize_mx(out=w_code[b][:].bitcast(FP8X4), scales=w_scale[b][:], in_=w_bf[:].rearrange("p m t -> p (m t)"))
 
@@ -94,7 +95,7 @@ def tile_picked_ygpr_relu_p_kernel(tc, x_words, x_scales, w1, gate, coef, offs, 
         for i, (lo, hi) in enumerate(((0, 256), (256, 384), (384, S))):
             if lo >= half:
                 nc.vector.tensor_copy(x_scale[1][:, lo - half : hi - half], all_scales[:].indirect(offs_sb[:, lo // 16 : hi // 16]))
-            acc = ps.tile([P, S], F32, name="acc%d" % i)
+            acc = ps.tile([P, S], F32, name="acc%d" % i, tag="bank%d" % i)
             project(acc, 0, lo, hi)
             if hi < S:
                 nc.scalar.activation(h[0][:, lo:hi], acc[:, lo:hi], RELU)
@@ -105,14 +106,13 @@ def tile_picked_ygpr_relu_p_kernel(tc, x_words, x_scales, w1, gate, coef, offs, 
         t1 = per_block(sb, "t1", [P, S], F32)
         t2 = per_block(sb, "t2", [P, S], F32)
         u1 = per_block(sb, "u1", [P, S], F32)
-        u2 = per_block(sb, "u2", [P, S], F32)
         h_c = per_block(sb, "h_c", [P, S], F32)
         gg_c = per_block(sb, "gg_c", [P, S], F32)
         gate_c = per_block(sb, "gate_c", [P, S], F32)
         turned_sb = per_block(sb, "turned_sb", [P, S], F32)
         res = per_block(sb, "res", [P, S], F32)
-        turned = [ps.tile([P, S], F32, name="turned%d" % b) for b in blocks]
-        partial = [ps.tile([P, S], F32, name="partial%d" % b) for b in blocks]
+        halves = range(2)
+        turned = [[ps.tile([P, half], F32, name="turned%d%d" % (b, i)) for i in halves] for b in blocks]
 
         def fetch(dst, window, pos, factor, lo=0, hi=S):
             nc.vector.tensor_tensor(dst[:, lo:hi], window[:].indirect(pos[:, lo // 16 : hi // 16]), factor[:, lo:hi], MULT)
@@ -120,22 +120,32 @@ def tile_picked_ygpr_relu_p_kernel(tc, x_words, x_scales, w1, gate, coef, offs, 
         def scaled(dst, src, b, depth):
             nc.scalar.activation(dst[:], src[:, 0:S], COPY, scale=coef_sb[:, b, depth : depth + 1])
 
-        def add_turned(b, term, first, last):
-            for c, cols in enumerate(chunks):
-                nc.tensor.matmul(turned[b][:, cols], term[:, cols], ident[:], is_transpose=True,
-                                 start=first and c == 0, stop=last and c == len(chunks) - 1)
+        def add_turned(b, term, first, last, parts=halves):
+            for i in parts:
+                for c in range(2):
+                    nc.tensor.matmul(turned[b][i][:, chunks[c]], term[:, chunks[2 * i + c]], ident[:], is_transpose=True,
+                                     start=first and c == 0, stop=last and c == 1)
 
-        def turn_back(b):
-            nc.scalar.copy(turned_sb[b][:], turned[b][:])
-            for cols in chunks:
-                nc.tensor.transpose(partial[b][:, cols], turned_sb[b][:, cols], ident[:])
+        partial = {}
 
-        def finish(b, lo, hi):
-            nc.vector.scalar_tensor_tensor(res[b][:, lo:hi], u2[b][:, lo:hi], coef_sb[:, b, 2:3], partial[b][:, lo:hi], MULT, ADD)
+        def turn_back(b, i):
+            nc.scalar.copy(turned_sb[b][:, i * half : (i + 1) * half], turned[b][i][:])
+            partial[b, i] = ps.tile([P, half], F32, name="partial%d%d" % (b, i), tag="bank%d" % (2 * b + i))
+            for c in range(2):
+                nc.tensor.transpose(partial[b, i][:, chunks[c]], turned_sb[b][:, chunks[2 * i + c]], ident[:])
+
+        def fetch_last(b, lo, hi, tag):
+            piece = sb.tile([P, hi - lo], F32, name="u2_%d_%d" % (b, lo), tag=tag, align_bytes=64)
+            nc.vector.tensor_tensor(piece[:], gg[b][:].indirect(pos2_sb[:, lo // 16 : hi // 16]), gates[1][:, lo:hi], MULT)
+            return piece
+
+        def finish(b, lo, hi, piece):
+            i = lo // half
+            nc.vector.scalar_tensor_tensor(res[b][:, lo:hi], piece[:], coef_sb[:, b, 2:3], partial[b, i][:, lo - i * half : hi - i * half], MULT, ADD)
             nc.sync.dma_start(out[b * P : (b + 1) * P, lo:hi], res[b][:, lo:hi])
 
         fetch(t1[0], h[0], pos1_sb, gates[0])
-        second = ps.tile([P, S], F32, name="second")
+        second = ps.tile([P, S], F32, name="second", tag="bank3")
         project(second, 1, 0, half)
         project(second, 1, half, S)
         nc.scalar.activation(h[1][:, 0:S], second[:], RELU)
@@ -151,18 +161,25 @@ def tile_picked_ygpr_relu_p_kernel(tc, x_words, x_scales, w1, gate, coef, offs, 
         add_turned(0, gg_c[0], False, False)
         fetch(t2[1], h[1], pos2_sb, gates[1])
         fetch(u1[0], gg[0], pos1_sb, gate_c[0], 0, half)
+        add_turned(0, u1[0], False, True, (0,))
+        turn_back(0, 0)
         nc.vector.tensor_tensor(gg[1][:, 0:S], t1[1][:], t2[1][:], ADD)
         scaled(gg_c[1], gg[1], 1, 1)
         add_turned(1, gg_c[1], False, False)
         fetch(u1[0], gg[0], pos1_sb, gate_c[0], half, S)
-        add_turned(0, u1[0], False, True)
+        add_turned(0, u1[0], False, True, (1,))
+        turn_back(0, 1)
         fetch(u1[1], gg[1], pos1_sb, gate_c[1])
         add_turned(1, u1[1], False, True)
-        turn_back(0)
-        turn_back(1)
-        fetch(u2[0], gg[0], pos2_sb, gates[1])
-        fetch(u2[1], gg[1], pos2_sb, gates[1], 0, half)
-        finish(0, 0, S)
-        fetch(u2[1], gg[1], pos2_sb, gates[1], half, S)
-        finish(1, 0, half)
-        finish(1, half, S)
+        turn_back(1, 0)
+        turn_back(1, 1)
+        a0 = fetch_last(0, 0, 256, "last0")
+        b0 = fetch_last(0, 256, 512, "last1")
+        a1 = fetch_last(1, 0, 256, "last2")
+        finish(0, 0, 256, a0)
+        finish(0, 256, 512, b0)
+        b1 = fetch_last(1, 256, 384, "last0")
+        finish(1, 0, 256, a1)
+        c1 = fetch_last(1, 384, 512, "last1")
+        finish(1, 256, 384, b1)
+        finish(1, 384, 512, c1)

@@ -6,7 +6,10 @@ from concourse.masks import make_identity
 K, T, S, N = 512, 1024, 512, 256
 P = 128
 PACK = 4
+STRIPE = 16
+HALF = S // 2
 PAD = 8
+PIECES = ((0, HALF), (HALF, HALF + P), (HALF + P, S))
 FLOPS = 2 * K * S * N
 
 F32 = mybir.dt.float32
@@ -22,24 +25,29 @@ RELU = mybir.ActivationFunctionType.Relu
 COPY = mybir.ActivationFunctionType.Copy
 
 
+def entries(list_tile, lo, hi):
+    return list_tile[:, lo // STRIPE : hi // STRIPE]
+
+
 def tile_picked_ygpr_relu_p_kernel(tc, x_words, x_scales, w1, gate, coef, offs, pos1, pos2, out):
     nc = tc.nc
     blocks = range(N // P)
+    halves = range(S // HALF)
     chunks = [slice(c * P, (c + 1) * P) for c in range(S // P)]
 
     with ExitStack() as ctx:
         sb = ctx.enter_context(tc.tile_pool(name="sb", bufs=1))
         ps = ctx.enter_context(tc.psum_pool(name="ps", bufs=1))
 
-        def per_block(pool, name, shape, dtype):
-            return [pool.tile(shape, dtype, name="%s%d" % (name, b), align_bytes=64) for b in blocks]
+        def per_block(name, shape, dtype):
+            return [sb.tile(shape, dtype, name="%s%d" % (name, b), align_bytes=64) for b in blocks]
 
-        offs_sb = sb.tile([P, S // 16], U16, name="offs_sb")
-        pos1_sb = sb.tile([P, S // 16], U16, name="pos1_sb")
-        pos2_sb = sb.tile([P, S // 16], U16, name="pos2_sb")
+        offs_sb = sb.tile([P, S // STRIPE], U16, name="offs_sb")
+        pos1_sb = sb.tile([P, S // STRIPE], U16, name="pos1_sb")
+        pos2_sb = sb.tile([P, S // STRIPE], U16, name="pos2_sb")
         all_scales = sb.tile([P, T], U8, name="all_scales", align_bytes=64)
         all_words = sb.tile([P, T], I32, name="all_words", align_bytes=64)
-        w_raw = per_block(sb, "w_raw", [P, PACK, P], F32)
+        w_raw = [sb.tile([P, PACK, P], F32, name="w_raw%d" % b, tag="raw%d" % b, align_bytes=64) for b in blocks]
         gate_sb = sb.tile([P, 2, S], F32, name="gate_sb", align_bytes=64)
         gates = [gate_sb[:, d, :] for d in range(2)]
         coef_sb = sb.tile([P, N // P, 3], F32, name="coef_sb")
@@ -56,130 +64,138 @@ def tile_picked_ygpr_relu_p_kernel(tc, x_words, x_scales, w1, gate, coef, offs, 
             nc.sync.dma_start(all_scales[32 * q : 32 * q + 4, :].bitcast(I32), x_scales[0, 4 * q : 4 * q + 4, :].bitcast(I32))
         for b in blocks:
             nc.sync.dma_start(w_raw[b][:], w1.rearrange("(p j) n -> p j n", j=PACK)[:, :, b * P : (b + 1) * P])
+        nc.sync.dma_start(gate_sb[:], gate.rearrange("d p s -> p d s"))
         nc.sync.dma_start(pos1_sb[:], pos1)
         nc.sync.dma_start(pos2_sb[:], pos2)
-        nc.sync.dma_start(gate_sb[:], gate.rearrange("d p s -> p d s"))
 
-        h = per_block(sb, "h", [P, S + PAD], F32)
-        gg = per_block(sb, "gg", [P, S + PAD], F32)
+        h = per_block("h", [P, S + PAD], F32)
+        gg = per_block("gg", [P, S + PAD], F32)
         for window in h + gg:
             nc.scalar.activation(window[:, S:], zeros[:], RELU)
 
         x_code = sb.tile([P, S], U32, name="x_code", align_bytes=64)
         nc.vector.tensor_copy(x_code[:], all_words[:].bitcast(U32).indirect(offs_sb[:]))
 
-        w_code = per_block(sb, "w_code", [P, P], U32)
-        w_scale = per_block(sb, "w_scale", [P, P], U8)
+        w_code = per_block("w_code", [P, P], U32)
+        w_scale = per_block("w_scale", [P, P], U8)
 
         def quantise(b):
-            w_bf = sb.tile([P, P, PACK], BF16, name="w_bf%d" % b, tag="staging%d" % b, align_bytes=64)
+            w_bf = sb.tile([P, P, PACK], BF16, name="w_bf%d" % b, align_bytes=64)
             nc.scalar.copy(
                 w_bf[:].rearrange("p (c i) t -> p c t i", i=4),
                 w_raw[b][:].rearrange("p t (c i) -> p c t i", i=4),
             )
             nc.vector.quantize_mx(out=w_code[b][:].bitcast(FP8X4), scales=w_scale[b][:], in_=w_bf[:].rearrange("p m t -> p (m t)"))
 
-        half = S // 2
-        x_scale = [sb.tile([P, half], U8, name="x_scale0", align_bytes=64)]
-        nc.vector.tensor_copy(x_scale[0][:], all_scales[:].indirect(offs_sb[:, 0 : half // 16]))
+        x_scale = [sb.tile([P, HALF], U8, name="x_scale0", align_bytes=64)]
+        nc.vector.tensor_copy(x_scale[0][:], all_scales[:].indirect(entries(offs_sb, 0, HALF)))
         quantise(0)
-        x_scale.append(sb.tile([P, half], U8, name="x_scale1", tag="staging0", align_bytes=64))
+        x_scale.append(sb.tile([P, HALF], U8, name="x_scale1", tag="raw0", align_bytes=64))
 
         def project(acc, b, lo, hi):
-            part = lo // half
+            i = lo // HALF
             nc.tensor.matmul_mx(
-                out=acc[:, lo:hi], lhsT=w_code[b][:].bitcast(FP8X4), lhsT_scale=w_scale[b][:],
-                rhs=x_code[:, lo:hi].bitcast(FP8X4), rhs_scale=x_scale[part][:, lo - part * half : hi - part * half], start=True, stop=True,
+                out=acc[:, lo:hi],
+                lhsT=w_code[b][:].bitcast(FP8X4),
+                lhsT_scale=w_scale[b][:],
+                rhs=x_code[:, lo:hi].bitcast(FP8X4),
+                rhs_scale=x_scale[i][:, lo - i * HALF : hi - i * HALF],
+                start=True,
+                stop=True,
             )
 
-        for i, (lo, hi) in enumerate(((0, 256), (256, 384), (384, S))):
-            if lo >= half:
-                nc.vector.tensor_copy(x_scale[1][:, lo - half : hi - half], all_scales[:].indirect(offs_sb[:, lo // 16 : hi // 16]))
-            acc = ps.tile([P, S], F32, name="acc%d" % i, tag="bank%d" % i)
+        for n, (lo, hi) in enumerate(PIECES):
+            if lo >= HALF:
+                nc.vector.tensor_copy(x_scale[1][:, lo - HALF : hi - HALF], all_scales[:].indirect(entries(offs_sb, lo, hi)))
+            acc = ps.tile([P, S], F32, name="acc%d" % n, tag="bank%d" % n)
             project(acc, 0, lo, hi)
-            if hi < S:
-                nc.scalar.activation(h[0][:, lo:hi], acc[:, lo:hi], RELU)
-            else:
-                quantise(1)
-                nc.vector.tensor_scalar_max(h[0][:, lo:hi], acc[:, lo:hi], 0.0)
+            nc.scalar.activation(h[0][:, lo:hi], acc[:, lo:hi], RELU)
+        quantise(1)
 
-        t1 = per_block(sb, "t1", [P, S], F32)
-        t2 = per_block(sb, "t2", [P, S], F32)
-        u1 = per_block(sb, "u1", [P, S], F32)
-        h_c = per_block(sb, "h_c", [P, S], F32)
-        gg_c = per_block(sb, "gg_c", [P, S], F32)
-        gate_c = per_block(sb, "gate_c", [P, S], F32)
-        turned_sb = per_block(sb, "turned_sb", [P, S], F32)
-        res = per_block(sb, "res", [P, S], F32)
-        halves = range(2)
-        turned = [[ps.tile([P, half], F32, name="turned%d%d" % (b, i)) for i in halves] for b in blocks]
-
-        def fetch(dst, window, pos, factor, lo=0, hi=S):
-            nc.vector.tensor_tensor(dst[:, lo:hi], window[:].indirect(pos[:, lo // 16 : hi // 16]), factor[:, lo:hi], MULT)
-
-        def scaled(dst, src, b, depth):
-            nc.scalar.activation(dst[:], src[:, 0:S], COPY, scale=coef_sb[:, b, depth : depth + 1])
-
-        def add_turned(b, term, first, last, parts=halves):
-            for i in parts:
-                for c in range(2):
-                    nc.tensor.matmul(turned[b][i][:, chunks[c]], term[:, chunks[2 * i + c]], ident[:], is_transpose=True,
-                                     start=first and c == 0, stop=last and c == 1)
-
+        h_p0 = per_block("h_p0", [P, S], F32)
+        h_p1 = per_block("h_p1", [P, S], F32)
+        gg_p0 = per_block("gg_p0", [P, S], F32)
+        h_c = per_block("h_c", [P, S], F32)
+        gg_c = per_block("gg_c", [P, S], F32)
+        gate0_c = per_block("gate0_c", [P, S], F32)
+        turned_sb = per_block("turned_sb", [P, S], F32)
+        res = per_block("res", [P, S], F32)
+        turned = [[ps.tile([P, HALF], F32, name="turned%d%d" % (b, i)) for i in halves] for b in blocks]
         partial = {}
 
+        def fetch(dst, window, pos, factor, lo, hi):
+            nc.vector.tensor_tensor(dst, window[:].indirect(entries(pos, lo, hi)), factor, MULT)
+
+        def fetch_columns(dst, window, pos, factor, lo=0, hi=S):
+            fetch(dst[:, lo:hi], window, pos, factor[:, lo:hi], lo, hi)
+
+        def scaled(dst, src, b, depth):
+            nc.scalar.activation(dst, src, COPY, scale=coef_sb[:, b, depth : depth + 1])
+
+        def add_turned(b, term, parts, first=False, last=False):
+            for i in parts:
+                for c in range(2):
+                    nc.tensor.matmul(
+                        turned[b][i][:, chunks[c]], term[:, chunks[2 * i + c]], ident[:], is_transpose=True,
+                        start=first and c == 0, stop=last and c == 1,
+                    )
+
         def turn_back(b, i):
-            nc.scalar.copy(turned_sb[b][:, i * half : (i + 1) * half], turned[b][i][:])
-            partial[b, i] = ps.tile([P, half], F32, name="partial%d%d" % (b, i), tag="bank%d" % (2 * b + i))
+            nc.scalar.copy(turned_sb[b][:, i * HALF : (i + 1) * HALF], turned[b][i][:])
+            partial[b, i] = ps.tile([P, HALF], F32, name="partial%d%d" % (b, i), tag="bank%d" % (2 * b + i))
             for c in range(2):
                 nc.tensor.transpose(partial[b, i][:, chunks[c]], turned_sb[b][:, chunks[2 * i + c]], ident[:])
 
-        def fetch_last(b, lo, hi, tag):
-            piece = sb.tile([P, hi - lo], F32, name="u2_%d_%d" % (b, lo), tag=tag, align_bytes=64)
-            nc.vector.tensor_tensor(piece[:], gg[b][:].indirect(pos2_sb[:, lo // 16 : hi // 16]), gates[1][:, lo:hi], MULT)
-            return piece
-
-        def finish(b, lo, hi, piece):
-            i = lo // half
-            nc.vector.scalar_tensor_tensor(res[b][:, lo:hi], piece[:], coef_sb[:, b, 2:3], partial[b, i][:, lo - i * half : hi - i * half], MULT, ADD)
+        def store(b, lo, hi):
             nc.sync.dma_start(out[b * P : (b + 1) * P, lo:hi], res[b][:, lo:hi])
 
-        fetch(t1[0], h[0], pos1_sb, gates[0])
-        second = ps.tile([P, S], F32, name="second", tag="bank3")
-        project(second, 1, 0, half)
-        project(second, 1, half, S)
-        nc.scalar.activation(h[1][:, 0:S], second[:], RELU)
-        fetch(t2[0], h[0], pos2_sb, gates[1])
+        def finish(b, lo, hi, last_term):
+            i = lo // HALF
+            nc.vector.scalar_tensor_tensor(res[b][:, lo:hi], last_term, coef_sb[:, b, 2:3], partial[b, i][:, lo - i * HALF : hi - i * HALF], MULT, ADD)
+            store(b, lo, hi)
+
+        fetch_columns(h_p0[0], h[0], pos1_sb, gates[0])
+        acc = ps.tile([P, S], F32, name="acc_block1", tag="bank%d" % len(PIECES))
+        for i in halves:
+            project(acc, 1, i * HALF, (i + 1) * HALF)
+        nc.scalar.activation(h[1][:, 0:S], acc[:], RELU)
+        fetch_columns(h_p1[0], h[0], pos2_sb, gates[1])
         for b in blocks:
-            scaled(gate_c[b], gates[0], b, 2)
+            scaled(gate0_c[b][:], gates[0], b, 2)
+        gate1_c = sb.tile([P, HALF], F32, name="gate1_c", align_bytes=64)
+        scaled(gate1_c[:], gates[1][:, 0:HALF], 0, 2)
         for b in blocks:
-            scaled(h_c[b], h[b], b, 0)
-            add_turned(b, h_c[b], True, False)
-        fetch(t1[1], h[1], pos1_sb, gates[0])
-        nc.vector.tensor_tensor(gg[0][:, 0:S], t1[0][:], t2[0][:], ADD)
-        scaled(gg_c[0], gg[0], 0, 1)
-        add_turned(0, gg_c[0], False, False)
-        fetch(t2[1], h[1], pos2_sb, gates[1])
-        fetch(u1[0], gg[0], pos1_sb, gate_c[0], 0, half)
-        add_turned(0, u1[0], False, True, (0,))
+            scaled(h_c[b][:], h[b][:, 0:S], b, 0)
+            add_turned(b, h_c[b], halves, first=True)
+        fetch_columns(h_p0[1], h[1], pos1_sb, gates[0])
+        nc.vector.tensor_tensor(gg[0][:, 0:S], h_p0[0][:], h_p1[0][:], ADD)
+        scaled(gg_c[0][:], gg[0][:, 0:S], 0, 1)
+        add_turned(0, gg_c[0], halves)
+        fetch_columns(h_p1[1], h[1], pos2_sb, gates[1])
+
+        fetch_columns(gg_p0[0], gg[0], pos1_sb, gate0_c[0], 0, HALF)
+        add_turned(0, gg_p0[0], (0,))
+        nc.vector.tensor_tensor(gg[1][:, 0:S], h_p0[1][:], h_p1[1][:], ADD)
+        scaled(gg_c[1][:], gg[1][:, 0:S], 1, 1)
+        add_turned(1, gg_c[1], halves)
+        early_term = sb.tile([P, HALF], F32, name="early_term", align_bytes=64)
+        fetch(early_term[:], gg[0], pos2_sb, gate1_c[:], 0, HALF)
+        add_turned(0, early_term, (0,), last=True)
         turn_back(0, 0)
-        nc.vector.tensor_tensor(gg[1][:, 0:S], t1[1][:], t2[1][:], ADD)
-        scaled(gg_c[1], gg[1], 1, 1)
-        add_turned(1, gg_c[1], False, False)
-        fetch(u1[0], gg[0], pos1_sb, gate_c[0], half, S)
-        add_turned(0, u1[0], False, True, (1,))
+        nc.scalar.copy(res[0][:, 0:HALF], partial[0, 0][:])
+        store(0, 0, HALF)
+        fetch_columns(gg_p0[0], gg[0], pos1_sb, gate0_c[0], HALF, S)
+        add_turned(0, gg_p0[0], (1,), last=True)
         turn_back(0, 1)
-        fetch(u1[1], gg[1], pos1_sb, gate_c[1])
-        add_turned(1, u1[1], False, True)
-        turn_back(1, 0)
-        turn_back(1, 1)
-        a0 = fetch_last(0, 0, 256, "last0")
-        b0 = fetch_last(0, 256, 512, "last1")
-        a1 = fetch_last(1, 0, 256, "last2")
-        finish(0, 0, 256, a0)
-        finish(0, 256, 512, b0)
-        b1 = fetch_last(1, 256, 384, "last0")
-        finish(1, 0, 256, a1)
-        c1 = fetch_last(1, 384, 512, "last1")
-        finish(1, 256, 384, b1)
-        finish(1, 384, 512, c1)
+        for i in halves:
+            fetch_columns(gg_p0[1], gg[1], pos1_sb, gate0_c[1], i * HALF, (i + 1) * HALF)
+            add_turned(1, gg_p0[1], (i,), last=True)
+            turn_back(1, i)
+
+        late_term0 = sb.tile([P, HALF], F32, name="late_term0", align_bytes=64)
+        fetch(late_term0[:], gg[0], pos2_sb, gates[1][:, HALF:S], HALF, S)
+        late_term1 = sb.tile([P, S], F32, name="late_term1", align_bytes=64)
+        fetch_columns(late_term1, gg[1], pos2_sb, gates[1])
+        finish(0, HALF, S, late_term0[:])
+        for lo, hi in PIECES:
+            finish(1, lo, hi, late_term1[:, lo:hi])

@@ -118,9 +118,10 @@ def tile_picked_ygpr_relu_p_kernel(tc, x_words, x_scales, w1, gate, coef, offs, 
         h_c = per_block("h_c", [P, S], F32)
         gg_c = per_block("gg_c", [P, S], F32)
         gate0_c = per_block("gate0_c", [P, S], F32)
-        turned_sb = per_block("turned_sb", [P, S], F32)
-        res = per_block("res", [P, S], F32)
-        turned = [[ps.tile([P, HALF], F32, name="turned%d%d" % (b, i)) for i in halves] for b in blocks]
+        parts = [((0, HALF), (HALF, S)), PIECES]
+        turned_tag = {(0, 0): "turned0", (0, 1): "turned1", (1, 0): "turned2", (1, 1): "turned3", (1, 2): "turned0"}
+        partial_tag = {(0, 0): "bank2", (0, 1): "bank3", (1, 0): "bank0", (1, 1): "bank1", (1, 2): "bank2"}
+        turned = {}
         partial = {}
 
         def fetch(dst, window, pos, factor, lo, hi):
@@ -132,70 +133,102 @@ def tile_picked_ygpr_relu_p_kernel(tc, x_words, x_scales, w1, gate, coef, offs, 
         def scaled(dst, src, b, depth):
             nc.scalar.activation(dst, src, COPY, scale=coef_sb[:, b, depth : depth + 1])
 
-        def add_turned(b, term, parts, first=False, last=False):
-            for i in parts:
-                for c in range(2):
+        def add_turned(b, term, which, first=False, last=False, base=0):
+            for i in which:
+                lo, hi = parts[b][i]
+                if first:
+                    turned[b, i] = ps.tile([P, hi - lo], F32, name="turned%d%d" % (b, i), tag=turned_tag[b, i])
+                for c in range(lo, hi, P):
                     nc.tensor.matmul(
-                        turned[b][i][:, chunks[c]], term[:, chunks[2 * i + c]], ident[:], is_transpose=True,
-                        start=first and c == 0, stop=last and c == 1,
+                        turned[b, i][:, c - lo : c - lo + P], term[:, c - base : c - base + P], ident[:], is_transpose=True,
+                        start=first and c == lo, stop=last and c + P == hi,
                     )
 
-        def turn_back(b, i):
-            nc.scalar.copy(turned_sb[b][:, i * HALF : (i + 1) * HALF], turned[b][i][:])
-            partial[b, i] = ps.tile([P, HALF], F32, name="partial%d%d" % (b, i), tag="bank%d" % (2 * b + i))
+        def turn_back(b, i, tag=None):
+            lo, hi = parts[b][i]
+            name = "turned_sb%d%d" % (b, i)
+            staged = sb.tile([P, hi - lo], F32, name=name, tag=tag or name, align_bytes=64)
+            nc.scalar.copy(staged[:], turned[b, i][:])
+            partial[b, i] = ps.tile([P, hi - lo], F32, name="partial%d%d" % (b, i), tag=partial_tag[b, i])
+            for c in range(0, hi - lo, P):
+                nc.tensor.transpose(partial[b, i][:, c : c + P], staged[:, c : c + P], ident[:])
+
+        def copy_out(i, tag):
+            lo, hi = parts[0][i]
+            res = sb.tile([P, hi - lo], F32, name="res0%d" % i, tag=tag, align_bytes=64)
+            nc.scalar.copy(res[:], partial[0, i][:])
+            nc.sync.dma_start(out[0:P, lo:hi], res[:])
+
+        def finish(i, last_term):
+            lo, hi = parts[1][i]
+            res = sb.tile([P, hi - lo], F32, name="res1%d" % i, align_bytes=64)
+            nc.vector.scalar_tensor_tensor(res[:], last_term[:, lo:hi], coef_sb[:, 1, 2:3], partial[1, i][:], MULT, ADD)
+            nc.sync.dma_start(out[P : 2 * P, lo:hi], res[:])
+
+        gate1_c = sb.tile([P, S], F32, name="gate1_c", align_bytes=64)
+        gg_turned_sb = per_block("gg_turned_sb", [P, HALF], F32)
+
+        def sum_turned(b, bank, term, first):
             for c in range(2):
-                nc.tensor.transpose(partial[b, i][:, chunks[c]], turned_sb[b][:, chunks[2 * i + c]], ident[:])
+                nc.tensor.matmul(bank[:, chunks[c]], term[:, chunks[c]], ident[:], is_transpose=True, start=first and c == 0, stop=not first and c == 1)
 
-        def store(b, lo, hi):
-            nc.sync.dma_start(out[b * P : (b + 1) * P, lo:hi], res[b][:, lo:hi])
-
-        def finish(b, lo, hi, last_term):
-            i = lo // HALF
-            nc.vector.scalar_tensor_tensor(res[b][:, lo:hi], last_term, coef_sb[:, b, 2:3], partial[b, i][:, lo - i * HALF : hi - i * HALF], MULT, ADD)
-            store(b, lo, hi)
+        def first_round(b):
+            bank = ps.tile([P, HALF], F32, name="gg_turned%d" % b, tag="bank0")
+            sum_turned(b, bank, h_p0[b], True)
+            fetch_columns(h_p1[b], h[b], pos2_sb, gates[1], HALF, S)
+            fetch_columns(h_p1[b], h[b], pos2_sb, gates[1], 0, HALF)
+            sum_turned(b, bank, h_p1[b], False)
+            nc.vector.tensor_tensor(gg[b][:, HALF:S], h_p0[b][:, HALF:S], h_p1[b][:, HALF:S], ADD)
+            nc.scalar.copy(gg_turned_sb[b][:], bank[:])
+            back = ps.tile([P, HALF], F32, name="gg_back%d" % b, tag="bank1")
+            for c in range(2):
+                nc.tensor.transpose(back[:, chunks[c]], gg_turned_sb[b][:, chunks[c]], ident[:])
+            return back
 
         fetch_columns(h_p0[0], h[0], pos1_sb, gates[0])
-        acc = ps.tile([P, S], F32, name="acc_block1", tag="bank%d" % len(PIECES))
+        acc = ps.tile([P, S], F32, name="acc_block1", tag="bank3")
         for i in halves:
             project(acc, 1, i * HALF, (i + 1) * HALF)
         nc.scalar.activation(h[1][:, 0:S], acc[:], RELU)
-        fetch_columns(h_p1[0], h[0], pos2_sb, gates[1])
-        for b in blocks:
-            scaled(gate0_c[b][:], gates[0], b, 2)
-        gate1_c = sb.tile([P, HALF], F32, name="gate1_c", align_bytes=64)
-        scaled(gate1_c[:], gates[1][:, 0:HALF], 0, 2)
-        for b in blocks:
-            scaled(h_c[b][:], h[b][:, 0:S], b, 0)
-            add_turned(b, h_c[b], halves, first=True)
-        fetch_columns(h_p0[1], h[1], pos1_sb, gates[0])
-        nc.vector.tensor_tensor(gg[0][:, 0:S], h_p0[0][:], h_p1[0][:], ADD)
+        scaled(gate0_c[0][:], gates[0], 0, 2)
+        scaled(gate1_c[:], gates[1], 0, 2)
+        scaled(h_c[0][:], h[0][:, 0:S], 0, 0)
+        add_turned(0, h_c[0], halves, first=True)
+        back = first_round(0)
+        scaled(h_c[1][:], h[1][:, 0:S], 1, 0)
+        nc.scalar.copy(gg[0][:, 0:HALF], back[:])
+        add_turned(1, h_c[1], (0, 1), first=True)
         scaled(gg_c[0][:], gg[0][:, 0:S], 0, 1)
+        scaled(gate0_c[1][:], gates[0], 1, 2)
+        fetch_columns(h_p0[1], h[1], pos1_sb, gates[0])
         add_turned(0, gg_c[0], halves)
-        fetch_columns(h_p1[1], h[1], pos2_sb, gates[1])
-
-        fetch_columns(gg_p0[0], gg[0], pos1_sb, gate0_c[0], 0, HALF)
-        add_turned(0, gg_p0[0], (0,))
-        nc.vector.tensor_tensor(gg[1][:, 0:S], h_p0[1][:], h_p1[1][:], ADD)
+        back = first_round(1)
+        nc.scalar.copy(gg[1][:, 0:HALF], back[:])
         scaled(gg_c[1][:], gg[1][:, 0:S], 1, 1)
-        add_turned(1, gg_c[1], halves)
-        early_term = sb.tile([P, HALF], F32, name="early_term", align_bytes=64)
-        fetch(early_term[:], gg[0], pos2_sb, gate1_c[:], 0, HALF)
-        add_turned(0, early_term, (0,), last=True)
-        turn_back(0, 0)
-        nc.scalar.copy(res[0][:, 0:HALF], partial[0, 0][:])
-        store(0, 0, HALF)
-        fetch_columns(gg_p0[0], gg[0], pos1_sb, gate0_c[0], HALF, S)
-        add_turned(0, gg_p0[0], (1,), last=True)
-        turn_back(0, 1)
-        for i in halves:
-            fetch_columns(gg_p0[1], gg[1], pos1_sb, gate0_c[1], i * HALF, (i + 1) * HALF)
-            add_turned(1, gg_p0[1], (i,), last=True)
-            turn_back(1, i)
 
-        late_term0 = sb.tile([P, HALF], F32, name="late_term0", align_bytes=64)
-        fetch(late_term0[:], gg[0], pos2_sb, gates[1][:, HALF:S], HALF, S)
+        gg_p1 = sb.tile([P, S], F32, name="gg_p1", align_bytes=64)
+        for i in halves:
+            fetch_columns(gg_p0[0], gg[0], pos1_sb, gate0_c[0], i * HALF, (i + 1) * HALF)
+            add_turned(0, gg_p0[0], (i,))
+            fetch_columns(gg_p1, gg[0], pos2_sb, gate1_c, i * HALF, (i + 1) * HALF)
+            add_turned(0, gg_p1, (i,), last=True)
+            if i == 0:
+                add_turned(1, gg_c[1], (0, 1))
+                turn_back(0, 0)
+        add_turned(1, h_c[1], (2,), first=True)
+        add_turned(1, gg_c[1], (2,))
+        copy_out(0, "res00")
+        for i, (lo, hi) in enumerate(PIECES):
+            term = sb.tile([P, hi - lo], F32, name="term%d" % i, tag="term%d" % i, align_bytes=64)
+            fetch(term[:], gg[1], pos1_sb, gate0_c[1][:, lo:hi], lo, hi)
+            add_turned(1, term, (i,), last=True, base=lo)
+            turn_back(1, i)
+            if i == 0:
+                turn_back(0, 1, tag="term0")
+        copy_out(1, "term2")
+
         late_term1 = sb.tile([P, S], F32, name="late_term1", align_bytes=64)
-        fetch_columns(late_term1, gg[1], pos2_sb, gates[1])
-        finish(0, HALF, S, late_term0[:])
-        for lo, hi in PIECES:
-            finish(1, lo, hi, late_term1[:, lo:hi])
+        for i in halves:
+            fetch_columns(late_term1, gg[1], pos2_sb, gates[1], i * HALF, (i + 1) * HALF)
+        for i in range(len(PIECES)):
+            finish(i, late_term1)

@@ -10,6 +10,7 @@ STRIPE = 16
 HALF = S // 2
 PAD = 8
 PIECES = ((0, HALF), (HALF, HALF + P), (HALF + P, S))
+TURNED = (HALF, P)
 FLOPS = 2 * K * S * N
 
 F32 = mybir.dt.float32
@@ -117,10 +118,9 @@ def tile_picked_ygpr_relu_p_kernel(tc, x_words, x_scales, w1, gate, coef, offs, 
         gg_p0 = per_block("gg_p0", [P, S], F32)
         h_c = per_block("h_c", [P, S], F32)
         gg_c = per_block("gg_c", [P, S], F32)
-        gate0_c = per_block("gate0_c", [P, S], F32)
-        parts = [((0, HALF), (HALF, S)), PIECES]
-        turned_tag = {(0, 0): "turned0", (0, 1): "turned1", (1, 0): "turned2", (1, 1): "turned3", (1, 2): "turned0"}
-        partial_tag = {(0, 0): "bank2", (0, 1): "bank3", (1, 0): "bank0", (1, 1): "bank1", (1, 2): "bank2"}
+        parts = [((0, HALF), (HALF, S))] * 2
+        turned_tag = {(0, 0): "turned0", (0, 1): "turned1", (1, 0): "turned2", (1, 1): "turned3"}
+        partial_tag = {(0, 0): "bank2", (0, 1): "bank3", (1, 0): "bank0", (1, 1): "bank1"}
         turned = {}
         partial = {}
 
@@ -159,30 +159,37 @@ def tile_picked_ygpr_relu_p_kernel(tc, x_words, x_scales, w1, gate, coef, offs, 
             nc.scalar.copy(res[:], partial[0, i][:])
             nc.sync.dma_start(out[0:P, lo:hi], res[:])
 
-        def finish(i, last_term):
-            lo, hi = parts[1][i]
-            res = sb.tile([P, hi - lo], F32, name="res1%d" % i, align_bytes=64)
-            nc.vector.scalar_tensor_tensor(res[:], last_term[:, lo:hi], coef_sb[:, 1, 2:3], partial[1, i][:], MULT, ADD)
-            nc.sync.dma_start(out[P : 2 * P, lo:hi], res[:])
+        def finish(b, lo, hi, last_term):
+            i = lo // HALF
+            res = sb.tile([P, hi - lo], F32, name="res%d_%d" % (b, lo), align_bytes=64)
+            nc.vector.scalar_tensor_tensor(res[:], last_term, coef_sb[:, b, 2:3], partial[b, i][:, lo - i * HALF : hi - i * HALF], MULT, ADD)
+            nc.sync.dma_start(out[b * P : (b + 1) * P, lo:hi], res[:])
 
-        gate1_c = sb.tile([P, S], F32, name="gate1_c", align_bytes=64)
-        gg_turned_sb = per_block("gg_turned_sb", [P, HALF], F32)
-
-        def sum_turned(b, bank, term, first):
-            for c in range(2):
-                nc.tensor.matmul(bank[:, chunks[c]], term[:, chunks[c]], ident[:], is_transpose=True, start=first and c == 0, stop=not first and c == 1)
+        gate1_c = sb.tile([P, HALF], F32, name="gate1_c", align_bytes=64)
+        gate0_c = {}
+        for b in blocks:
+            for i in halves:
+                gate0_c[b, i] = sb.tile([P, HALF], F32, name="gate0_c%d%d" % (b, i), tag="gate0_c%d%d" % (b, i), align_bytes=64)
+                nc.vector.tensor_scalar(gate0_c[b, i][:], gates[0][:, i * HALF : (i + 1) * HALF], coef_sb[:, b, 2:3], None, MULT)
+        nc.vector.tensor_scalar(gate1_c[:], gates[1][:, 0:HALF], coef_sb[:, 0, 2:3], None, MULT)
 
         def first_round(b):
-            bank = ps.tile([P, HALF], F32, name="gg_turned%d" % b, tag="bank0")
-            sum_turned(b, bank, h_p0[b], True)
-            fetch_columns(h_p1[b], h[b], pos2_sb, gates[1], HALF, S)
-            fetch_columns(h_p1[b], h[b], pos2_sb, gates[1], 0, HALF)
-            sum_turned(b, bank, h_p1[b], False)
-            nc.vector.tensor_tensor(gg[b][:, HALF:S], h_p0[b][:, HALF:S], h_p1[b][:, HALF:S], ADD)
-            nc.scalar.copy(gg_turned_sb[b][:], bank[:])
-            back = ps.tile([P, HALF], F32, name="gg_back%d" % b, tag="bank1")
-            for c in range(2):
-                nc.tensor.transpose(back[:, chunks[c]], gg_turned_sb[b][:, chunks[c]], ident[:])
+            width = TURNED[b]
+            bank = ps.tile([P, width], F32, name="gg_turned%d" % b, tag="bank0")
+            for c in range(0, width, P):
+                nc.tensor.matmul(bank[:, c : c + P], h_p0[b][:, c : c + P], ident[:], is_transpose=True, start=c == 0, stop=False)
+            rest = ((width, S - P), (S - P, S))
+            for lo, hi in ((0, width),) + rest:
+                fetch_columns(h_p1[b], h[b], pos2_sb, gates[1], lo, hi)
+            for c in range(0, width, P):
+                nc.tensor.matmul(bank[:, c : c + P], h_p1[b][:, c : c + P], ident[:], is_transpose=True, start=False, stop=c + P == width)
+            for lo, hi in rest:
+                nc.vector.tensor_tensor(gg[b][:, lo:hi], h_p0[b][:, lo:hi], h_p1[b][:, lo:hi], ADD)
+            staged = sb.tile([P, width], F32, name="gg_turned_sb%d" % b, align_bytes=64)
+            nc.scalar.copy(staged[:], bank[:])
+            back = ps.tile([P, width], F32, name="gg_back%d" % b, tag="bank1")
+            for c in range(0, width, P):
+                nc.tensor.transpose(back[:, c : c + P], staged[:, c : c + P], ident[:])
             return back
 
         fetch_columns(h_p0[0], h[0], pos1_sb, gates[0])
@@ -190,45 +197,38 @@ def tile_picked_ygpr_relu_p_kernel(tc, x_words, x_scales, w1, gate, coef, offs, 
         for i in halves:
             project(acc, 1, i * HALF, (i + 1) * HALF)
         nc.scalar.activation(h[1][:, 0:S], acc[:], RELU)
-        scaled(gate0_c[0][:], gates[0], 0, 2)
-        scaled(gate1_c[:], gates[1], 0, 2)
         scaled(h_c[0][:], h[0][:, 0:S], 0, 0)
         add_turned(0, h_c[0], halves, first=True)
         back = first_round(0)
         scaled(h_c[1][:], h[1][:, 0:S], 1, 0)
-        nc.scalar.copy(gg[0][:, 0:HALF], back[:])
+        nc.scalar.copy(gg[0][:, 0 : TURNED[0]], back[:])
         add_turned(1, h_c[1], (0, 1), first=True)
         scaled(gg_c[0][:], gg[0][:, 0:S], 0, 1)
-        scaled(gate0_c[1][:], gates[0], 1, 2)
         fetch_columns(h_p0[1], h[1], pos1_sb, gates[0])
         add_turned(0, gg_c[0], halves)
         back = first_round(1)
-        nc.scalar.copy(gg[1][:, 0:HALF], back[:])
+        nc.scalar.copy(gg[1][:, 0 : TURNED[1]], back[:])
         scaled(gg_c[1][:], gg[1][:, 0:S], 1, 1)
 
-        gg_p1 = sb.tile([P, S], F32, name="gg_p1", align_bytes=64)
-        for i in halves:
-            fetch_columns(gg_p0[0], gg[0], pos1_sb, gate0_c[0], i * HALF, (i + 1) * HALF)
-            add_turned(0, gg_p0[0], (i,))
-            fetch_columns(gg_p1, gg[0], pos2_sb, gate1_c, i * HALF, (i + 1) * HALF)
-            add_turned(0, gg_p1, (i,), last=True)
-            if i == 0:
-                add_turned(1, gg_c[1], (0, 1))
-                turn_back(0, 0)
-        add_turned(1, h_c[1], (2,), first=True)
-        add_turned(1, gg_c[1], (2,))
+        fetch(gg_p0[0][:, 0:HALF], gg[0], pos1_sb, gate0_c[0, 0][:], 0, HALF)
+        add_turned(0, gg_p0[0], (0,))
+        early_term = sb.tile([P, HALF], F32, name="early_term", align_bytes=64)
+        fetch(early_term[:], gg[0], pos2_sb, gate1_c[:], 0, HALF)
+        add_turned(0, early_term, (0,), last=True)
+        add_turned(1, gg_c[1], halves)
+        turn_back(0, 0)
+        fetch(gg_p0[0][:, HALF:S], gg[0], pos1_sb, gate0_c[0, 1][:], HALF, S)
+        add_turned(0, gg_p0[0], (1,), last=True)
+        turn_back(0, 1)
         copy_out(0, "res00")
-        for i, (lo, hi) in enumerate(PIECES):
-            term = sb.tile([P, hi - lo], F32, name="term%d" % i, tag="term%d" % i, align_bytes=64)
-            fetch(term[:], gg[1], pos1_sb, gate0_c[1][:, lo:hi], lo, hi)
-            add_turned(1, term, (i,), last=True, base=lo)
-            turn_back(1, i)
-            if i == 0:
-                turn_back(0, 1, tag="term0")
-        copy_out(1, "term2")
-
-        late_term1 = sb.tile([P, S], F32, name="late_term1", align_bytes=64)
         for i in halves:
-            fetch_columns(late_term1, gg[1], pos2_sb, gates[1], i * HALF, (i + 1) * HALF)
-        for i in range(len(PIECES)):
-            finish(i, late_term1)
+            fetch(gg_p0[1][:, i * HALF : (i + 1) * HALF], gg[1], pos1_sb, gate0_c[1, i][:], i * HALF, (i + 1) * HALF)
+            add_turned(1, gg_p0[1], (i,), last=True)
+            turn_back(1, i)
+        late_term0 = sb.tile([P, HALF], F32, name="late_term0", tag="gate0_c10", align_bytes=64)
+        fetch(late_term0[:], gg[0], pos2_sb, gates[1][:, HALF:S], HALF, S)
+        late_term1 = sb.tile([P, S], F32, name="late_term1", align_bytes=64)
+        fetch_columns(late_term1, gg[1], pos2_sb, gates[1])
+        finish(0, HALF, S, late_term0[:])
+        for lo, hi in PIECES:
+            finish(1, lo, hi, late_term1[:, lo:hi])

@@ -10,7 +10,6 @@ STRIPE = 16
 HALF = S // 2
 PAD = 8
 PIECES = ((0, HALF), (HALF, HALF + P), (HALF + P, S))
-TURNED = (HALF, P)
 FLOPS = 2 * K * S * N
 
 F32 = mybir.dt.float32
@@ -59,8 +58,8 @@ def tile_picked_ygpr_relu_p_kernel(tc, x_words, x_scales, w1, gate, coef, offs, 
         nc.gpsimd.memset(zeros[:], 0.0)
         make_identity(nc, ident[:])
         nc.gpsimd.dma_start(coef_sb[:], coef.rearrange("(b p) c -> p b c", p=P))
-        nc.sync.dma_start(offs_sb[:], offs)
         nc.sync.dma_start(all_words[:], x_words[0].rearrange("p n t -> p (n t)").bitcast(I32))
+        nc.sync.dma_start(offs_sb[:], offs)
         for q in range(4):
             nc.sync.dma_start(all_scales[32 * q : 32 * q + 4, :].bitcast(I32), x_scales[0, 4 * q : 4 * q + 4, :].bitcast(I32))
         for b in blocks:
@@ -173,24 +172,30 @@ def tile_picked_ygpr_relu_p_kernel(tc, x_words, x_scales, w1, gate, coef, offs, 
                 nc.vector.tensor_scalar(gate0_c[b, i][:], gates[0][:, i * HALF : (i + 1) * HALF], coef_sb[:, b, 2:3], None, MULT)
         nc.vector.tensor_scalar(gate1_c[:], gates[1][:, 0:HALF], coef_sb[:, 0, 2:3], None, MULT)
 
-        def first_round(b):
-            width = TURNED[b]
-            bank = ps.tile([P, width], F32, name="gg_turned%d" % b, tag="bank0")
-            for c in range(0, width, P):
-                nc.tensor.matmul(bank[:, c : c + P], h_p0[b][:, c : c + P], ident[:], is_transpose=True, start=c == 0, stop=False)
-            rest = ((width, S - P), (S - P, S))
-            for lo, hi in ((0, width),) + rest:
+        def first_round(b, order, turned_pieces):
+            banks = {}
+            for n, (lo, hi) in enumerate(turned_pieces):
+                banks[lo] = ps.tile([P, hi - lo], F32, name="gg_turned%d%d" % (b, n), tag="bank%d" % n)
+                for c in range(lo, hi, P):
+                    nc.tensor.matmul(banks[lo][:, c - lo : c - lo + P], h_p0[b][:, c : c + P], ident[:], is_transpose=True, start=c == lo, stop=False)
+            for lo, hi in order:
                 fetch_columns(h_p1[b], h[b], pos2_sb, gates[1], lo, hi)
-            for c in range(0, width, P):
-                nc.tensor.matmul(bank[:, c : c + P], h_p1[b][:, c : c + P], ident[:], is_transpose=True, start=False, stop=c + P == width)
-            for lo, hi in rest:
-                nc.vector.tensor_tensor(gg[b][:, lo:hi], h_p0[b][:, lo:hi], h_p1[b][:, lo:hi], ADD)
-            staged = sb.tile([P, width], F32, name="gg_turned_sb%d" % b, align_bytes=64)
-            nc.scalar.copy(staged[:], bank[:])
-            back = ps.tile([P, width], F32, name="gg_back%d" % b, tag="bank1")
-            for c in range(0, width, P):
-                nc.tensor.transpose(back[:, c : c + P], staged[:, c : c + P], ident[:])
-            return back
+                if lo in banks:
+                    for c in range(lo, hi, P):
+                        nc.tensor.matmul(banks[lo][:, c - lo : c - lo + P], h_p1[b][:, c : c + P], ident[:], is_transpose=True, start=False, stop=c + P == hi)
+            for lo, hi in order:
+                if lo not in banks:
+                    nc.vector.tensor_tensor(gg[b][:, lo:hi], h_p0[b][:, lo:hi], h_p1[b][:, lo:hi], ADD)
+            backs = []
+            for n, (lo, hi) in enumerate(turned_pieces):
+                staged = sb.tile([P, hi - lo], F32, name="gg_turned_sb%d%d" % (b, n), align_bytes=64)
+                nc.scalar.copy(staged[:], banks[lo][:])
+                back = ps.tile([P, hi - lo], F32, name="gg_back%d%d" % (b, n), tag="bank%d" % (2 + n))
+                backs.append(back)
+                for c in range(0, hi - lo, P):
+                    nc.tensor.transpose(back[:, c : c + P], staged[:, c : c + P], ident[:])
+            for n, (lo, hi) in enumerate(turned_pieces):
+                nc.scalar.copy(gg[b][:, lo:hi], backs[n][:])
 
         fetch_columns(h_p0[0], h[0], pos1_sb, gates[0])
         acc = ps.tile([P, S], F32, name="acc_block1", tag="bank3")
@@ -199,15 +204,13 @@ def tile_picked_ygpr_relu_p_kernel(tc, x_words, x_scales, w1, gate, coef, offs, 
         nc.scalar.activation(h[1][:, 0:S], acc[:], RELU)
         scaled(h_c[0][:], h[0][:, 0:S], 0, 0)
         add_turned(0, h_c[0], halves, first=True)
-        back = first_round(0)
         scaled(h_c[1][:], h[1][:, 0:S], 1, 0)
-        nc.scalar.copy(gg[0][:, 0 : TURNED[0]], back[:])
+        first_round(0, (PIECES[0], PIECES[2], PIECES[1]), PIECES[:2])
         add_turned(1, h_c[1], (0, 1), first=True)
         scaled(gg_c[0][:], gg[0][:, 0:S], 0, 1)
         fetch_columns(h_p0[1], h[1], pos1_sb, gates[0])
         add_turned(0, gg_c[0], halves)
-        back = first_round(1)
-        nc.scalar.copy(gg[1][:, 0 : TURNED[1]], back[:])
+        first_round(1, ((0, P), (P, S - P), (S - P, S)), ((0, P),))
         scaled(gg_c[1][:], gg[1][:, 0:S], 1, 1)
 
         fetch(gg_p0[0][:, 0:HALF], gg[0], pos1_sb, gate0_c[0, 0][:], 0, HALF)

@@ -48,8 +48,7 @@ def tile_picked_ygpr_relu_p_kernel(tc, x_words, x_scales, w1, gate, coef, offs, 
         all_scales = sb.tile([P, T], U8, name="all_scales", align_bytes=64)
         all_words = sb.tile([P, T], I32, name="all_words", align_bytes=64)
         w_raw = [sb.tile([P, PACK, P], F32, name="w_raw%d" % b, tag="raw%d" % b, align_bytes=64) for b in blocks]
-        gate_sb = sb.tile([P, 2, S], F32, name="gate_sb", align_bytes=64)
-        gates = [gate_sb[:, d, :] for d in range(2)]
+        gates = [sb.tile([P, S], F32, name="gate%d" % d, align_bytes=64)[:] for d in range(2)]
         coef_sb = sb.tile([P, N // P, 3], F32, name="coef_sb")
         zeros = sb.tile([P, PAD], F32, name="zeros")
         ident = sb.tile([P, P], F32, name="ident", align_bytes=64)
@@ -64,9 +63,10 @@ def tile_picked_ygpr_relu_p_kernel(tc, x_words, x_scales, w1, gate, coef, offs, 
             nc.sync.dma_start(all_scales[32 * q : 32 * q + 4, :].bitcast(I32), x_scales[0, 4 * q : 4 * q + 4, :].bitcast(I32))
         for b in blocks:
             nc.sync.dma_start(w_raw[b][:], w1.rearrange("(p j) n -> p j n", j=PACK)[:, :, b * P : (b + 1) * P])
-        nc.sync.dma_start(gate_sb[:], gate.rearrange("d p s -> p d s"))
-        nc.sync.dma_start(pos1_sb[:], pos1)
+        nc.sync.dma_start(gates[0], gate[0])
         nc.sync.dma_start(pos2_sb[:], pos2)
+        nc.sync.dma_start(pos1_sb[:], pos1)
+        nc.sync.dma_start(gates[1], gate[1])
 
         h = per_block("h", [P, S + PAD], F32)
         gg = per_block("gg", [P, S + PAD], F32)
@@ -112,126 +112,122 @@ def tile_picked_ygpr_relu_p_kernel(tc, x_words, x_scales, w1, gate, coef, offs, 
             nc.scalar.activation(h[0][:, lo:hi], acc[:, lo:hi], RELU)
         quantise(1)
 
-        h_p0 = per_block("h_p0", [P, S], F32)
-        h_p1 = per_block("h_p1", [P, S], F32)
-        gg_p0 = per_block("gg_p0", [P, S], F32)
-        h_c = per_block("h_c", [P, S], F32)
-        gg_c = per_block("gg_c", [P, S], F32)
-        parts = [((0, HALF), (HALF, S))] * 2
-        turned_tag = {(0, 0): "turned0", (0, 1): "turned1", (1, 0): "turned2", (1, 1): "turned3"}
-        partial_tag = {(0, 0): "bank2", (0, 1): "bank3", (1, 0): "bank0", (1, 1): "bank1"}
+        halves_of = [(i * HALF, (i + 1) * HALF) for i in halves]
+        near0 = per_block("near0", [P, S], F32)
+        near1 = per_block("near1", [P, S], F32)
+        near1_g = per_block("near1_g", [P, S], F32)
+        far0 = per_block("far0", [P, S], F32)
+        far1 = per_block("far1", [P, S], F32)
+        far1_g = per_block("far1_g", [P, S], F32)
+        far0_plain = sb.tile([P, S], F32, name="far0_plain", align_bytes=64)
+        h_c = sb.tile([P, S], F32, name="h_c", align_bytes=64)
+        gg_c = sb.tile([P, S], F32, name="gg_c", align_bytes=64)
+        gate0_c = sb.tile([P, S], F32, name="gate0_c", align_bytes=64)
+        sum_h = sb.tile([P, S], F32, name="sum_h", align_bytes=64)
+        sum_gg = sb.tile([P, S], F32, name="sum_gg", align_bytes=64)
+        far_cut = S - 256
+        wide = 128
+        direct = S - 0
+        h_c1 = sb.tile([P, S], F32, name="h_c1", align_bytes=64)
+        gg_c1 = sb.tile([P, wide], F32, name="gg_c1", align_bytes=64)
+        gate0_c1 = sb.tile([P, wide], F32, name="gate0_c1", align_bytes=64)
+        turned1 = ps.tile([P, wide], F32, name="turned_block1")
         turned = {}
-        partial = {}
 
-        def fetch(dst, window, pos, factor, lo, hi):
-            nc.vector.tensor_tensor(dst, window[:].indirect(entries(pos, lo, hi)), factor, MULT)
+        def add_turned1(term, first=False, last=False):
+            for c in range(0, wide, P):
+                nc.tensor.matmul(turned1[:, c : c + P], term[:, c : c + P], ident[:], is_transpose=True, start=first and c == 0, stop=last and c + P == wide)
 
-        def fetch_columns(dst, window, pos, factor, lo=0, hi=S):
-            fetch(dst[:, lo:hi], window, pos, factor[:, lo:hi], lo, hi)
+        def fetch_times(dst, window, pos, factor, lo=0, hi=S):
+            nc.vector.tensor_tensor(dst[:, lo:hi], window[:].indirect(entries(pos, lo, hi)), factor[:, lo:hi], MULT)
+
+        def fetch_plain(dst, window, pos, lo=0, hi=S):
+            nc.scalar.activation(dst[:, lo:hi], window[:].indirect(entries(pos, lo, hi)), COPY)
 
         def scaled(dst, src, b, depth):
             nc.scalar.activation(dst, src, COPY, scale=coef_sb[:, b, depth : depth + 1])
 
-        def add_turned(b, term, which, first=False, last=False, base=0):
+        def add_turned(term, which, first=False, last=False, upto=S):
             for i in which:
-                lo, hi = parts[b][i]
+                lo, hi = halves_of[i]
+                hi = min(hi, upto)
                 if first:
-                    turned[b, i] = ps.tile([P, hi - lo], F32, name="turned%d%d" % (b, i), tag=turned_tag[b, i])
+                    turned[i] = ps.tile([P, HALF], F32, name="turned%d" % i)
                 for c in range(lo, hi, P):
                     nc.tensor.matmul(
-                        turned[b, i][:, c - lo : c - lo + P], term[:, c - base : c - base + P], ident[:], is_transpose=True,
+                        turned[i][:, c - lo : c - lo + P], term[:, c : c + P], ident[:], is_transpose=True,
                         start=first and c == lo, stop=last and c + P == hi,
                     )
 
-        def turn_back(b, i, tag=None):
-            lo, hi = parts[b][i]
-            name = "turned_sb%d%d" % (b, i)
-            staged = sb.tile([P, hi - lo], F32, name=name, tag=tag or name, align_bytes=64)
-            nc.scalar.copy(staged[:], turned[b, i][:])
-            partial[b, i] = ps.tile([P, hi - lo], F32, name="partial%d%d" % (b, i), tag=partial_tag[b, i])
-            for c in range(0, hi - lo, P):
-                nc.tensor.transpose(partial[b, i][:, c : c + P], staged[:, c : c + P], ident[:])
+        def times_plus(dst, term, depth, rest, lo, hi, op=ADD, b=1):
+            nc.vector.scalar_tensor_tensor(dst, term[:, lo:hi], coef_sb[:, b, depth : depth + 1], rest[:, lo:hi], MULT, op)
 
-        def copy_out(i, tag):
-            lo, hi = parts[0][i]
-            res = sb.tile([P, hi - lo], F32, name="res0%d" % i, tag=tag, align_bytes=64)
-            nc.scalar.copy(res[:], partial[0, i][:])
-            nc.sync.dma_start(out[0:P, lo:hi], res[:])
+        nc.vector.tensor_scalar(gate0_c[:], gates[0], coef_sb[:, 0, 2:3], None, MULT)
+        nc.vector.tensor_scalar(gate0_c1[:], gates[0][:, 0:wide], coef_sb[:, 1, 2:3], None, MULT)
+        for lo, hi in PIECES[:2]:
+            nc.vector.tensor_scalar(h_c[:, lo:hi], h[0][:, lo:hi], coef_sb[:, 0, 0:1], None, MULT)
+        acc_lo = ps.tile([P, HALF], F32, name="acc_block1_lo", tag="bank3")
+        acc_hi = ps.tile([P, S], F32, name="acc_block1_hi")
+        project(acc_lo, 1, 0, HALF)
+        project(acc_hi, 1, HALF, S)
+        nc.scalar.activation(h[1][:, 0:HALF], acc_lo[:], RELU)
+        nc.scalar.activation(h[1][:, HALF:S], acc_hi[:, HALF:S], RELU)
 
-        def finish(b, lo, hi, last_term):
-            i = lo // HALF
-            res = sb.tile([P, hi - lo], F32, name="res%d_%d" % (b, lo), align_bytes=64)
-            nc.vector.scalar_tensor_tensor(res[:], last_term, coef_sb[:, b, 2:3], partial[b, i][:, lo - i * HALF : hi - i * HALF], MULT, ADD)
-            nc.sync.dma_start(out[b * P : (b + 1) * P, lo:hi], res[:])
+        fetch_times(near0[0], h[0], pos1_sb, gates[0])
+        fetch_plain(near1[0], h[0], pos2_sb)
+        fetch_times(near0[1], h[1], pos1_sb, gates[0])
+        fetch_plain(near1[1], h[1], pos2_sb)
+        for lo, hi in halves_of:
+            nc.vector.tensor_tensor(near1_g[0][:, lo:hi], near1[0][:, lo:hi], gates[1][:, lo:hi], MULT)
+        for lo, hi in halves_of:
+            nc.vector.tensor_tensor(gg[0][:, lo:hi], near0[0][:, lo:hi], near1_g[0][:, lo:hi], ADD)
+        nc.vector.tensor_tensor(near1_g[1][:], near1[1][:], gates[1], MULT)
+        scaled(h_c[:, S - P : S], h[0][:, S - P : S], 0, 0)
+        add_turned(h_c, halves, first=True)
+        scaled(h_c1[:], h[1][:, 0:S], 1, 0)
+        add_turned1(h_c1, first=True)
+        scaled(gg_c[:], gg[0][:, 0:S], 0, 1)
+        add_turned(gg_c, halves)
+        fetch_plain(far1[0], gg[0], pos2_sb)
+        fetch_times(far0[0], gg[0], pos1_sb, gate0_c, 0, HALF)
+        add_turned(far0[0], (0,))
+        nc.vector.tensor_tensor(gg[1][:, 0:S], near0[1][:], near1_g[1][:], ADD)
+        fetch_times(far0[0], gg[0], pos1_sb, gate0_c, HALF, S)
+        add_turned(far0[0], (1,))
+        times_plus(far1_g[0][:], far1[0], 2, gates[1], 0, S, MULT, 0)
+        add_turned(far1_g[0], halves, last=True, upto=direct)
+        scaled(gg_c1[:], gg[1][:, 0:wide], 1, 1)
+        add_turned1(gg_c1)
+        fetch_times(far0[1], gg[1], pos1_sb, gate0_c1, 0, wide)
+        add_turned1(far0[1], last=True)
+        times_plus(sum_h[:, wide:S], gg[1], 1, h_c1, wide, S)
+        fetch_plain(far1[1], gg[1], pos2_sb)
+        fetch_plain(far0_plain, gg[1], pos1_sb, far_cut, S)
+        fetch_times(far0[1], gg[1], pos1_sb, gates[0], wide, far_cut)
 
-        gate1_c = sb.tile([P, HALF], F32, name="gate1_c", align_bytes=64)
-        gate0_c = {}
-        for b in blocks:
-            for i in halves:
-                gate0_c[b, i] = sb.tile([P, HALF], F32, name="gate0_c%d%d" % (b, i), tag="gate0_c%d%d" % (b, i), align_bytes=64)
-                nc.vector.tensor_scalar(gate0_c[b, i][:], gates[0][:, i * HALF : (i + 1) * HALF], coef_sb[:, b, 2:3], None, MULT)
-        nc.vector.tensor_scalar(gate1_c[:], gates[1][:, 0:HALF], coef_sb[:, 0, 2:3], None, MULT)
+        def turn_back(summed, width, name, tag):
+            staged = sb.tile([P, width], F32, name="staged" + name, align_bytes=64)
+            nc.scalar.copy(staged[:], summed[:])
+            back = ps.tile([P, width], F32, name="back" + name, tag=tag)
+            for c in range(0, width, P):
+                nc.tensor.transpose(back[:, c : c + P], staged[:, c : c + P], ident[:])
+            return back
 
-        def first_round(b, order, turned_pieces):
-            banks = {}
-            for n, (lo, hi) in enumerate(turned_pieces):
-                banks[lo] = ps.tile([P, hi - lo], F32, name="gg_turned%d%d" % (b, n), tag="bank%d" % n)
-                for c in range(lo, hi, P):
-                    nc.tensor.matmul(banks[lo][:, c - lo : c - lo + P], h_p0[b][:, c : c + P], ident[:], is_transpose=True, start=c == lo, stop=False)
-            for lo, hi in order:
-                fetch_columns(h_p1[b], h[b], pos2_sb, gates[1], lo, hi)
-                if lo in banks:
-                    for c in range(lo, hi, P):
-                        nc.tensor.matmul(banks[lo][:, c - lo : c - lo + P], h_p1[b][:, c : c + P], ident[:], is_transpose=True, start=False, stop=c + P == hi)
-            for lo, hi in order:
-                if lo not in banks:
-                    nc.vector.tensor_tensor(gg[b][:, lo:hi], h_p0[b][:, lo:hi], h_p1[b][:, lo:hi], ADD)
-            backs = []
-            for n, (lo, hi) in enumerate(turned_pieces):
-                staged = sb.tile([P, hi - lo], F32, name="gg_turned_sb%d%d" % (b, n), align_bytes=64)
-                nc.scalar.copy(staged[:], banks[lo][:])
-                back = ps.tile([P, hi - lo], F32, name="gg_back%d%d" % (b, n), tag="bank%d" % (2 + n))
-                backs.append(back)
-                for c in range(0, hi - lo, P):
-                    nc.tensor.transpose(back[:, c : c + P], staged[:, c : c + P], ident[:])
-            for n, (lo, hi) in enumerate(turned_pieces):
-                nc.scalar.copy(gg[b][:, lo:hi], backs[n][:])
-
-        fetch_columns(h_p0[0], h[0], pos1_sb, gates[0])
-        acc = ps.tile([P, S], F32, name="acc_block1", tag="bank3")
-        for i in halves:
-            project(acc, 1, i * HALF, (i + 1) * HALF)
-        nc.scalar.activation(h[1][:, 0:S], acc[:], RELU)
-        scaled(h_c[0][:], h[0][:, 0:S], 0, 0)
-        add_turned(0, h_c[0], halves, first=True)
-        scaled(h_c[1][:], h[1][:, 0:S], 1, 0)
-        first_round(0, (PIECES[0], PIECES[2], PIECES[1]), PIECES[:2])
-        add_turned(1, h_c[1], (0, 1), first=True)
-        scaled(gg_c[0][:], gg[0][:, 0:S], 0, 1)
-        fetch_columns(h_p0[1], h[1], pos1_sb, gates[0])
-        add_turned(0, gg_c[0], halves)
-        first_round(1, ((0, P), (P, S - P), (S - P, S)), ((0, P),))
-        scaled(gg_c[1][:], gg[1][:, 0:S], 1, 1)
-
-        fetch(gg_p0[0][:, 0:HALF], gg[0], pos1_sb, gate0_c[0, 0][:], 0, HALF)
-        add_turned(0, gg_p0[0], (0,))
-        early_term = sb.tile([P, HALF], F32, name="early_term", align_bytes=64)
-        fetch(early_term[:], gg[0], pos2_sb, gate1_c[:], 0, HALF)
-        add_turned(0, early_term, (0,), last=True)
-        add_turned(1, gg_c[1], halves)
-        turn_back(0, 0)
-        fetch(gg_p0[0][:, HALF:S], gg[0], pos1_sb, gate0_c[0, 1][:], HALF, S)
-        add_turned(0, gg_p0[0], (1,), last=True)
-        turn_back(0, 1)
-        copy_out(0, "res00")
-        for i in halves:
-            fetch(gg_p0[1][:, i * HALF : (i + 1) * HALF], gg[1], pos1_sb, gate0_c[1, i][:], i * HALF, (i + 1) * HALF)
-            add_turned(1, gg_p0[1], (i,), last=True)
-            turn_back(1, i)
-        late_term0 = sb.tile([P, HALF], F32, name="late_term0", tag="gate0_c10", align_bytes=64)
-        fetch(late_term0[:], gg[0], pos2_sb, gates[1][:, HALF:S], HALF, S)
-        late_term1 = sb.tile([P, S], F32, name="late_term1", align_bytes=64)
-        fetch_columns(late_term1, gg[1], pos2_sb, gates[1])
-        finish(0, HALF, S, late_term0[:])
-        for lo, hi in PIECES:
-            finish(1, lo, hi, late_term1[:, lo:hi])
+        back0 = [turn_back(turned[i], HALF, "0%d" % i, "bank%d" % i) for i in halves]
+        back1 = turn_back(turned1, wide, "1", "bank2")
+        res = [sb.tile([P, HALF], F32, name="res0%d" % i, align_bytes=64) for i in halves]
+        nc.scalar.copy(res[0][:], back0[0][:])
+        nc.sync.dma_start(out[0:P, 0:HALF], res[0][:])
+        nc.scalar.copy(res[1][:, 0 : direct - HALF], back0[1][:, 0 : direct - HALF])
+        nc.sync.dma_start(out[0:P, HALF:S], res[1][:])
+        times_plus(far1_g[1][:, wide:S], far1[1], 2, gates[1], wide, S, MULT)
+        nc.vector.tensor_tensor(far0[1][:, far_cut:S], far0_plain[:, far_cut:S], gates[0][:, far_cut:S], MULT)
+        nc.vector.tensor_tensor(sum_gg[:, wide:S], far1_g[1][:, wide:S], sum_h[:, wide:S], ADD)
+        times_plus(far1_g[1][:, 0:wide], far1[1], 2, gates[1], 0, wide, MULT)
+        for lo, hi in ((wide, S),):
+            last = sb.tile([P, hi - lo], F32, name="res1_%d" % lo, align_bytes=64)
+            times_plus(last[:], far0[1], 2, sum_gg, lo, hi)
+            nc.sync.dma_start(out[P : 2 * P, lo:hi], last[:])
+        res_wide = sb.tile([P, wide], F32, name="res_wide", align_bytes=64)
+        nc.vector.tensor_tensor(res_wide[:], far1_g[1][:, 0:wide], back1[:], ADD)
+        nc.sync.dma_start(out[P : 2 * P, 0:wide], res_wide[:])

@@ -125,7 +125,7 @@ def tile_picked_ygpr_relu_p_kernel(tc, x_words, x_scales, w1, gate, coef, offs, 
         gate0_c = sb.tile([P, S], F32, name="gate0_c", align_bytes=64)
         sum_h = sb.tile([P, S], F32, name="sum_h", align_bytes=64)
         sum_gg = sb.tile([P, S], F32, name="sum_gg", align_bytes=64)
-        far_cut = S - 256
+        far_cut = S - 128
         wide = 128
         direct = S - 0
         h_c1 = sb.tile([P, S], F32, name="h_c1", align_bytes=64)

from contextlib import ExitStack

import concourse.mybir as mybir
from concourse.masks import make_identity

K, T, S, N = 512, 1024, 512, 256
P = 128
PACK = 4
STRIPE = 16
HALF = S // 2
PAD = 8
PIECES = ((0, HALF), (HALF, HALF + P), (HALF + P, S))
FLOPS = 2 * K * S * N

F32 = mybir.dt.float32
BF16 = mybir.dt.bfloat16
I32 = mybir.dt.int32
U32 = mybir.dt.uint32
U16 = mybir.dt.uint16
U8 = mybir.dt.uint8
FP8X4 = mybir.dt.float8_e4m3fn_x4
MULT = mybir.AluOpType.mult
ADD = mybir.AluOpType.add
RELU = mybir.ActivationFunctionType.Relu
COPY = mybir.ActivationFunctionType.Copy


def entries(list_tile, lo, hi):
    return list_tile[:, lo // STRIPE : hi // STRIPE]


def tile_picked_ygpr_relu_p_kernel(tc, x_words, x_scales, w1, gate, coef, offs, pos1, pos2, out):
    nc = tc.nc
    blocks = range(N // P)
    halves = range(S // HALF)
    chunks = [slice(c * P, (c + 1) * P) for c in range(S // P)]

    with ExitStack() as ctx:
        sb = ctx.enter_context(tc.tile_pool(name="sb", bufs=1))
        ps = ctx.enter_context(tc.psum_pool(name="ps", bufs=1))

        def per_block(name, shape, dtype):
            return [sb.tile(shape, dtype, name="%s%d" % (name, b), align_bytes=64) for b in blocks]

        offs_sb = sb.tile([P, S // STRIPE], U16, name="offs_sb")
        pos1_sb = sb.tile([P, S // STRIPE], U16, name="pos1_sb")
        pos2_sb = sb.tile([P, S // STRIPE], U16, name="pos2_sb")
        all_scales = sb.tile([P, T], U8, name="all_scales", align_bytes=64)
        all_words = sb.tile([P, T], I32, name="all_words", align_bytes=64)
        w_raw = [sb.tile([P, PACK, P], F32, name="w_raw%d" % b, tag="raw%d" % b, align_bytes=64) for b in blocks]
        gates = [sb.tile([P, S], F32, name="gate%d" % d, align_bytes=64)[:] for d in range(2)]
        coef_sb = sb.tile([P, N // P, 3], F32, name="coef_sb")
        zeros = sb.tile([P, PAD], F32, name="zeros")
        ident = sb.tile([P, P], F32, name="ident", align_bytes=64)

        nc.gpsimd.memset(all_scales[:].bitcast(I32), 0)
        nc.gpsimd.memset(zeros[:], 0.0)
        make_identity(nc, ident[:])
        nc.gpsimd.dma_start(coef_sb[:], coef.rearrange("(b p) c -> p b c", p=P))
        nc.sync.dma_start(all_words[:], x_words[0].rearrange("p n t -> p (n t)").bitcast(I32))
        nc.sync.dma_start(offs_sb[:], offs)
        for q in range(4):
            nc.sync.dma_start(all_scales[32 * q : 32 * q + 4, :].bitcast(I32), x_scales[0, 4 * q : 4 * q + 4, :].bitcast(I32))
        for b in blocks:
            nc.sync.dma_start(w_raw[b][:], w1.rearrange("(p j) n -> p j n", j=PACK)[:, :, b * P : (b + 1) * P])
        nc.sync.dma_start(gates[0], gate[0])
        nc.sync.dma_start(pos2_sb[:], pos2)
        nc.sync.dma_start(pos1_sb[:], pos1)
        nc.sync.dma_start(gates[1], gate[1])

        h = per_block("h", [P, S + PAD], F32)
        gg = per_block("gg", [P, S + PAD], F32)
        for window in h + gg:
            nc.scalar.activation(window[:, S:], zeros[:], RELU)

        x_code = sb.tile([P, S], U32, name="x_code", align_bytes=64)
        nc.vector.tensor_copy(x_code[:], all_words[:].bitcast(U32).indirect(offs_sb[:]))

        w_code = per_block("w_code", [P, P], U32)
        w_scale = per_block("w_scale", [P, P], U8)

        def quantise(b):
            w_bf = sb.tile([P, P, PACK], BF16, name="w_bf%d" % b, align_bytes=64)
            nc.scalar.copy(
                w_bf[:].rearrange("p (c i) t -> p c t i", i=4),
                w_raw[b][:].rearrange("p t (c i) -> p c t i", i=4),
            )
            nc.vector.quantize_mx(out=w_code[b][:].bitcast(FP8X4), scales=w_scale[b][:], in_=w_bf[:].rearrange("p m t -> p (m t)"))

        x_scale = [sb.tile([P, HALF], U8, name="x_scale0", align_bytes=64)]
        nc.vector.tensor_copy(x_scale[0][:], all_scales[:].indirect(entries(offs_sb, 0, HALF)))
        quantise(0)
        x_scale.append(sb.tile([P, HALF], U8, name="x_scale1", tag="raw0", align_bytes=64))

        def project(acc, b, lo, hi):
            i = lo // HALF
            nc.tensor.matmul_mx(
                out=acc[:, lo:hi],
                lhsT=w_code[b][:].bitcast(FP8X4),
                lhsT_scale=w_scale[b][:],
                rhs=x_code[:, lo:hi].bitcast(FP8X4),
                rhs_scale=x_scale[i][:, lo - i * HALF : hi - i * HALF],
                start=True,
                stop=True,
            )

        for n, (lo, hi) in enumerate(PIECES):
            if lo >= HALF:
                nc.vector.tensor_copy(x_scale[1][:, lo - HALF : hi - HALF], all_scales[:].indirect(entries(offs_sb, lo, hi)))
            acc = ps.tile([P, S], F32, name="acc%d" % n, tag="bank%d" % n)
            project(acc, 0, lo, hi)
            nc.scalar.activation(h[0][:, lo:hi], acc[:, lo:hi], RELU)
        quantise(1)

        halves_of = [(i * HALF, (i + 1) * HALF) for i in halves]
        near0 = per_block("near0", [P, S], F32)
        near1 = per_block("near1", [P, S], F32)
        near1_g = per_block("near1_g", [P, S], F32)
        far0 = per_block("far0", [P, S], F32)
        far1 = per_block("far1", [P, S], F32)
        far1_g = per_block("far1_g", [P, S], F32)
        far0_plain = sb.tile([P, S], F32, name="far0_plain", align_bytes=64)
        h_c = sb.tile([P, S], F32, name="h_c", align_bytes=64)
        gg_c = sb.tile([P, S], F32, name="gg_c", align_bytes=64)
        gate0_c = sb.tile([P, S], F32, name="gate0_c", align_bytes=64)
        sum_h = sb.tile([P, S], F32, name="sum_h", align_bytes=64)
        sum_gg = sb.tile([P, S], F32, name="sum_gg", align_bytes=64)
        far_cut = S - 128
        wide = 128
        direct = S - 0
        h_c1 = sb.tile([P, S], F32, name="h_c1", align_bytes=64)
        gg_c1 = sb.tile([P, wide], F32, name="gg_c1", align_bytes=64)
        gate0_c1 = sb.tile([P, wide], F32, name="gate0_c1", align_bytes=64)
        turned1 = ps.tile([P, wide], F32, name="turned_block1")
        turned = {}

        def add_turned1(term, first=False, last=False):
            for c in range(0, wide, P):
                nc.tensor.matmul(turned1[:, c : c + P], term[:, c : c + P], ident[:], is_transpose=True, start=first and c == 0, stop=last and c + P == wide)

        def fetch_times(dst, window, pos, factor, lo=0, hi=S):
            nc.vector.tensor_tensor(dst[:, lo:hi], window[:].indirect(entries(pos, lo, hi)), factor[:, lo:hi], MULT)

        def fetch_plain(dst, window, pos, lo=0, hi=S):
            nc.scalar.activation(dst[:, lo:hi], window[:].indirect(entries(pos, lo, hi)), COPY)

        def scaled(dst, src, b, depth):
            nc.scalar.activation(dst, src, COPY, scale=coef_sb[:, b, depth : depth + 1])

        def add_turned(term, which, first=False, last=False, upto=S):
            for i in which:
                lo, hi = halves_of[i]
                hi = min(hi, upto)
                if first:
                    turned[i] = ps.tile([P, HALF], F32, name="turned%d" % i)
                for c in range(lo, hi, P):
                    nc.tensor.matmul(
                        turned[i][:, c - lo : c - lo + P], term[:, c : c + P], ident[:], is_transpose=True,
                        start=first and c == lo, stop=last and c + P == hi,
                    )

        def times_plus(dst, term, depth, rest, lo, hi, op=ADD, b=1):
            nc.vector.scalar_tensor_tensor(dst, term[:, lo:hi], coef_sb[:, b, depth : depth + 1], rest[:, lo:hi], MULT, op)

        nc.vector.tensor_scalar(gate0_c[:], gates[0], coef_sb[:, 0, 2:3], None, MULT)
        nc.vector.tensor_scalar(gate0_c1[:], gates[0][:, 0:wide], coef_sb[:, 1, 2:3], None, MULT)
        for lo, hi in PIECES[:2]:
            nc.vector.tensor_scalar(h_c[:, lo:hi], h[0][:, lo:hi], coef_sb[:, 0, 0:1], None, MULT)
        acc_lo = ps.tile([P, HALF], F32, name="acc_block1_lo", tag="bank3")
        acc_hi = ps.tile([P, S], F32, name="acc_block1_hi")
        project(acc_lo, 1, 0, HALF)
        project(acc_hi, 1, HALF, S)
        nc.scalar.activation(h[1][:, 0:HALF], acc_lo[:], RELU)
        nc.scalar.activation(h[1][:, HALF:S], acc_hi[:, HALF:S], RELU)

        fetch_times(near0[0], h[0], pos1_sb, gates[0])
        fetch_plain(near1[0], h[0], pos2_sb)
        fetch_times(near0[1], h[1], pos1_sb, gates[0])
        fetch_plain(near1[1], h[1], pos2_sb)
        for lo, hi in halves_of:
            nc.vector.tensor_tensor(near1_g[0][:, lo:hi], near1[0][:, lo:hi], gates[1][:, lo:hi], MULT)
        for lo, hi in halves_of:
            nc.vector.tensor_tensor(gg[0][:, lo:hi], near0[0][:, lo:hi], near1_g[0][:, lo:hi], ADD)
        nc.vector.tensor_tensor(near1_g[1][:], near1[1][:], gates[1], MULT)
        scaled(h_c[:, S - P : S], h[0][:, S - P : S], 0, 0)
        add_turned(h_c, halves, first=True)
        scaled(h_c1[:], h[1][:, 0:S], 1, 0)
        add_turned1(h_c1, first=True)
        scaled(gg_c[:], gg[0][:, 0:S], 0, 1)
        add_turned(gg_c, halves)
        fetch_plain(far1[0], gg[0], pos2_sb)
        fetch_times(far0[0], gg[0], pos1_sb, gate0_c, 0, HALF)
        add_turned(far0[0], (0,))
        nc.vector.tensor_tensor(gg[1][:, 0:S], near0[1][:], near1_g[1][:], ADD)
        fetch_times(far0[0], gg[0], pos1_sb, gate0_c, HALF, S)
        add_turned(far0[0], (1,))
        times_plus(far1_g[0][:], far1[0], 2, gates[1], 0, S, MULT, 0)
        add_turned(far1_g[0], halves, last=True, upto=direct)
        scaled(gg_c1[:], gg[1][:, 0:wide], 1, 1)
        add_turned1(gg_c1)
        fetch_times(far0[1], gg[1], pos1_sb, gate0_c1, 0, wide)
        add_turned1(far0[1], last=True)
        times_plus(sum_h[:, wide:S], gg[1], 1, h_c1, wide, S)
        fetch_plain(far1[1], gg[1], pos2_sb)
        fetch_plain(far0_plain, gg[1], pos1_sb, far_cut, S)
        fetch_times(far0[1], gg[1], pos1_sb, gates[0], wide, far_cut)

        def turn_back(summed, width, name, tag):
            staged = sb.tile([P, width], F32, name="staged" + name, align_bytes=64)
            nc.scalar.copy(staged[:], summed[:])
            back = ps.tile([P, width], F32, name="back" + name, tag=tag)
            for c in range(0, width, P):
                nc.tensor.transpose(back[:, c : c + P], staged[:, c : c + P], ident[:])
            return back

        back0 = [turn_back(turned[i], HALF, "0%d" % i, "bank%d" % i) for i in halves]
        back1 = turn_back(turned1, wide, "1", "bank2")
        res = [sb.tile([P, HALF], F32, name="res0%d" % i, align_bytes=64) for i in halves]
        nc.scalar.copy(res[0][:], back0[0][:])
        nc.sync.dma_start(out[0:P, 0:HALF], res[0][:])
        nc.scalar.copy(res[1][:, 0 : direct - HALF], back0[1][:, 0 : direct - HALF])
        nc.sync.dma_start(out[0:P, HALF:S], res[1][:])
        times_plus(far1_g[1][:, wide:S], far1[1], 2, gates[1], wide, S, MULT)
        nc.vector.tensor_tensor(far0[1][:, far_cut:S], far0_plain[:, far_cut:S], gates[0][:, far_cut:S], MULT)
        nc.vector.tensor_tensor(sum_gg[:, wide:S], far1_g[1][:, wide:S], sum_h[:, wide:S], ADD)
        times_plus(far1_g[1][:, 0:wide], far1[1], 2, gates[1], 0, wide, MULT)
        for lo, hi in ((wide, S),):
            last = sb.tile([P, hi - lo], F32, name="res1_%d" % lo, align_bytes=64)
            times_plus(last[:], far0[1], 2, sum_gg, lo, hi)
            nc.sync.dma_start(out[P : 2 * P, lo:hi], last[:])
        res_wide = sb.tile([P, wide], F32, name="res_wide", align_bytes=64)
        nc.vector.tensor_tensor(res_wide[:], far1_g[1][:, 0:wide], back1[:], ADD)
        nc.sync.dma_start(out[P : 2 * P, 0:wide], res_wide[:])
